import numpy as np
import ml_dtypes


def mxq(x, axis, fmt="e4m3"):
    dtype, down = {"e4m3": (ml_dtypes.float8_e4m3fn, 7), "e5m2": (ml_dtypes.float8_e5m2, 14)}[fmt]
    v = np.moveaxis(np.asarray(x, np.float32).astype(ml_dtypes.bfloat16).astype(np.float64), axis, -1)
    blocks = v.reshape(v.shape[:-1] + (-1, 32))
    amax = np.abs(blocks).max(-1, keepdims=True)
    byte = np.maximum(np.where(amax > 0, np.frexp(amax)[1] - 1 + 127, 0) - down, 1)
    scale = np.exp2(byte - 127.0)
    codes = (blocks / scale).astype(np.float32).astype(dtype).astype(np.float64)
    return np.moveaxis((codes * scale).reshape(v.shape), -1, axis)


WIDE = False


def mx_kscale(k):
    if not WIDE:
        return np.ones(k)
    levels = np.array([10, -10, 5, -5, 0])
    if k % 512:
        return np.exp2(np.random.permutation(np.resize(levels, k // 32))).repeat(32)
    a = np.empty((k // 512, 16))
    for p in range(k // 512):
        a[p, :8] = np.random.permutation(np.resize(levels, 8))
        for g in range(8):
            far = levels[np.abs(levels - a[p, g]) >= 10]
            a[p, g + 8] = far[np.random.randint(len(far))]
    return np.exp2(a.ravel()).repeat(32)


BF16 = ml_dtypes.bfloat16


def bf(x):
    return np.asarray(x, np.float32).astype(BF16)


def f64(x):
    return np.asarray(x).astype(np.float64)


N, D, K, L = 2048, 1024, 512, 2


def lobe(frames, weight, bias):
    return np.tanh((mxq(frames, 1, "e4m3") @ mxq(weight, 0, "e4m3")) + bias[None, :])


def center(features):
    return features - np.mean(features, axis=0, keepdims=True)


def draw0():
    s, u = mx_kscale(D), mx_kscale(D)
    t = mx_kscale(N)
    scale = 1.0 / np.sqrt(D)
    return {
        "x": bf(np.random.standard_normal((N, D)) * s),
        "y": bf(np.random.standard_normal((N, D)) * u),
        "w0": bf(np.random.standard_normal((D, K)) * scale / s[:, None]),
        "w1": bf(np.random.standard_normal((D, K)) * scale / u[:, None]),
        "b": bf(np.random.standard_normal((L, K)) * 0.5),
        "p": bf((1.0 + 0.25 * np.random.standard_normal(N)) * t),
        "a": bf((1.0 + 0.25 * np.random.standard_normal(N)) / t),
    }


def core(x, y, w0, w1, b, p, a):
    n = x.shape[0]
    bias = f64(b)
    f = lobe(f64(x), f64(w0), bias[0])
    g = lobe(f64(y), f64(w1), bias[1])
    fc = center(f)
    gc = center(g)
    fp = fc * f64(p)[:, None]
    ga = gc * f64(a)[:, None]
    return (mxq(fp, 0, "e4m3").T @ mxq(ga, 0, "e4m3")) / np.sqrt(n)


def e4m3fn_bytes(y):
    return np.clip(np.asarray(y, np.float64), -448.0, 448.0).astype(np.float32).astype(ml_dtypes.float8_e4m3fn).view(np.uint8)


def e4m3fn_values(b):
    return np.asarray(b, np.uint8).view(ml_dtypes.float8_e4m3fn).astype(np.float64)


def setup_inputs():
    d = draw0()
    x0 = np.asarray(d['y']).astype(np.float64)
    s = (np.max(np.abs(x0), axis=(0,), keepdims=True) / 448.0).astype(np.float32)
    out = {}
    for k, v in d.items():
        if k == 'y':
            out['y_bytes'] = e4m3fn_bytes(x0 / s.astype(np.float64))
            out['y_scale'] = s
        else:
            out[k] = v
    return out


def reference(x, y_bytes, y_scale, w0, w1, b, p, a):
    return core(x, e4m3fn_values(y_bytes) * y_scale.astype(np.float64), w0, w1, b, p, a)

@@ -1,0 +1,390 @@
+import math
+from contextlib import ExitStack
+
+import concourse.mybir as mybir
+from concourse.masks import make_identity
+
+N, D, K = 2048, 1024, 512
+FLOPS = 2 * (2 * N * D * K) + 2 * N * K * K
+
+F32 = mybir.dt.float32
+BF16 = mybir.dt.bfloat16
+U32 = mybir.dt.uint32
+U8 = mybir.dt.uint8
+FP8 = mybir.dt.float8_e4m3fn
+FP8X4 = mybir.dt.float8_e4m3fn_x4
+ALU = mybir.AluOpType
+ACT = mybir.ActivationFunctionType
+
+P = 128
+PASS = 512
+HALF = 256
+D_PASSES = D // PASS
+GROUPS = N // PASS
+CHUNKS = K // P
+F_MAP, G_MAP = 0, 1
+
+
+def tile_twolobeweightedkoopmancrossmoment_kernel(tc, x, y_bytes, y_scale, w0, w1, b, p, a, out):
+    nc = tc.nc
+    with ExitStack() as ctx:
+        keep = ctx.enter_context(tc.tile_pool(name="keep", bufs=1))
+        work = ctx.enter_context(tc.tile_pool(name="work", bufs=2))
+        psum = ctx.enter_context(tc.psum_pool(name="psum", bufs=8))
+        ctx.enter_context(tc.manual_schedule())
+
+        def new_bank():
+            return psum.tile([P, PASS], F32, name="bank")
+
+        def new_words(stream, bufs):
+            return work.tile([P, 1024], F32, name="words_" + stream, bufs=bufs, align_bytes=64)
+
+        def new_codes(stream, bufs):
+            codes = work.tile([P, PASS], U32, name="codes_" + stream, bufs=bufs, align_bytes=64)
+            scales = work.tile([P, PASS], U8, name="scales_" + stream, bufs=bufs, align_bytes=64)
+            return codes, scales
+
+        def new_wide(dtype, columns):
+            return work.tile([P, columns], dtype, name="wide", bufs=2 * CHUNKS, align_bytes=256)
+
+        def quantize(codes, scales, values):
+            nc.vector.quantize_mx(out=codes.bitcast(FP8X4), scales=scales, in_=values)
+
+        scale_cols = keep.tile([P, 8], F32)
+        bias_rows = keep.tile([8, P], BF16)
+        w_rows, x_rows, y_rows, row_weight = {}, {}, {}, {}
+
+        def load_w(fmap, j):
+            if j == 0:
+                both = new_wide(BF16, D_PASSES * 4 * K)
+                for i in range(D_PASSES):
+                    w_rows[fmap, i] = both[:, i * 4 * K : (i + 1) * 4 * K]
+            src = (w0, w1)[fmap][j * PASS : (j + 1) * PASS, :]
+            nc.sync.dma_start(out=w_rows[fmap, j][:], in_=src.rearrange("(p t) k -> p (t k)", t=4))
+
+        def load_x(h):
+            x_rows[h] = keep.tile([P, 2 * D], BF16, name="x_rows_%d" % h, align_bytes=256)
+            nc.sync.dma_start(out=x_rows[h][:], in_=x[h * HALF : (h + 1) * HALF, :].rearrange("(r u) d -> r (u d)", u=2))
+
+        def load_y(h):
+            y_rows[h] = keep.tile([P, 2 * D], U8, name="y_byte_rows_%d" % h, align_bytes=256)
+            nc.sync.dma_start(
+                out=y_rows[h][:], in_=y_bytes[h * HALF : (h + 1) * HALF, :].rearrange("(r u) d -> r (u d)", u=2)
+            )
+
+        def load_row_weight(fmap):
+            row_weight[fmap] = keep.tile([P, N], BF16, name="row_weight_%d" % fmap, align_bytes=256)
+            nc.sync.dma_start(out=row_weight[fmap][:], in_=(p, a)[fmap].partition_broadcast(P))
+
+        nc.sync.dma_start(out=scale_cols[:], in_=y_scale.rearrange("o (q i) -> q (o i)", i=8))
+        nc.sync.dma_start(out=bias_rows[:], in_=b.rearrange("l (c q) -> (l c) q", q=P))
+        load_y(0)
+        load_w(F_MAP, 0)
+        load_x(0)
+        load_y(1)
+        load_x(1)
+        load_w(F_MAP, 1)
+        for g in range(1, GROUPS):
+            load_x(2 * g)
+            load_y(g + 1)
+            load_x(2 * g + 1)
+        load_w(G_MAP, 0)
+        load_y(5)
+        load_w(G_MAP, 1)
+        load_y(6)
+        load_y(7)
+        load_row_weight(F_MAP)
+        load_row_weight(G_MAP)
+
+        ident = keep.tile([P, P], F32)
+        make_identity(nc, ident[:])
+        bias_square = keep.tile([P, P], F32)
+        nc.gpsimd.memset(bias_square[:], 0.0)
+        nc.scalar.activation(out=bias_square[0:8, :], in_=bias_rows[:], func=ACT.Copy)
+
+        scale_rows = keep.tile([P, D], F32)
+        for v in range(2):
+            bank = new_bank()
+            for i in range(4):
+                col = 4 * (i // 2) + 2 * v + i % 2
+                nc.tensor.transpose(
+                    bank[:, i * P : (i + 1) * P], scale_cols[:, col : col + 1].to_broadcast([P, P]), ident[:]
+                )
+            (nc.vector.tensor_copy, nc.scalar.copy)[v](
+                out=scale_rows[:, v * PASS : (v + 1) * PASS].rearrange("p (q i) -> p q i", i=4),
+                in_=bank[:].rearrange("p (i q) -> p q i", i=4),
+            )
+
+        bias = keep.tile([P, 8], F32)
+        bank = new_bank()
+        nc.tensor.transpose(bank[:, 0:P], bias_square[:], ident[:])
+        nc.scalar.copy(out=bias[:], in_=bank[:, 0:8])
+
+        w_words, w_mx = {}, {}
+
+        def interleave_w(fmap, j, copy):
+            w_words[fmap, j] = new_words("w", 2)
+            copy(
+                out=w_words[fmap, j][:].bitcast(BF16).rearrange("p (k t) -> p k t", t=4),
+                in_=w_rows[fmap, j][:].rearrange("p (t k) -> p k t", t=4),
+            )
+
+        def quantize_w(fmap, j):
+            codes = keep.tile([P, K], U32, name="w_codes_%d_%d" % (fmap, j), align_bytes=64)
+            scales = keep.tile([P, K], U8, name="w_scales_%d_%d" % (fmap, j), align_bytes=64)
+            quantize(codes[:], scales[:], w_words[fmap, j][:].bitcast(BF16))
+            w_mx[fmap, j] = (codes, scales)
+
+        y_values = {}
+
+        def widen_y(h):
+            y_values[h] = work.tile([P, 2 * D], BF16, name="values", bufs=5, align_bytes=64)
+            for u in range(2):
+                cols = slice(u * D, (u + 1) * D)
+                nc.vector.tensor_tensor(
+                    out=y_values[h][:, cols].rearrange("p (v m e) -> p v m e", v=2, e=2),
+                    in0=y_rows[h][:, cols].bitcast(FP8).rearrange("p (m v e) -> p v m e", v=2, e=2),
+                    in1=scale_rows[:].rearrange("p (v m e) -> p v m e", v=2, e=2),
+                    op=ALU.mult,
+                )
+
+        row_words = {}
+
+        def turn_rows(fmap, h):
+            g, side = divmod(h, 2)
+            source = (x_rows, y_values)[fmap][h][:].bitcast(F32)
+            for j in range(D_PASSES):
+                if side == 0:
+                    row_words[fmap, g, j] = new_words("xy"[fmap], 4)
+                bank = new_bank()
+                for u in range(2):
+                    for v in range(2):
+                        if fmap == F_MAP:
+                            first = 512 * u + 256 * j + v
+                            pairs = source[:, first : 512 * u + 256 * (j + 1) : 2]
+                        else:
+                            first = 512 * u + 256 * v + P * j
+                            pairs = source[:, first : first + P]
+                        nc.tensor.transpose(bank[:, (2 * u + v) * P : (2 * u + v + 1) * P], pairs, ident[:])
+                target = row_words[fmap, g, j][:].rearrange("p (u s r v) -> p u s r v", u=2, s=2, v=2)
+                nc.scalar.copy(out=target[:, :, side, :, :], in_=bank[:].rearrange("p (u v r) -> p u r v", u=2, v=2))
+
+        row_mx = {}
+
+        def quantize_rows(fmap, g):
+            for j in range(D_PASSES):
+                row_mx[fmap, g, j] = new_codes("xy"[fmap], (4, 8)[fmap])
+                codes, scales = row_mx[fmap, g, j]
+                quantize(codes[:], scales[:], row_words[fmap, g, j][:].bitcast(BF16))
+
+        features = {}
+        sums = keep.tile([P, 2 * CHUNKS * GROUPS], F32)
+        means = keep.tile([P, 2 * CHUNKS], F32)
+
+        def feature_chunk(fmap, g, c):
+            cols = slice(c * P, (c + 1) * P)
+            bank = new_bank()
+            for j in range(D_PASSES):
+                w_codes, w_scales = w_mx[fmap, j]
+                codes, scales = row_mx[fmap, g, j]
+                nc.tensor.matmul_mx(
+                    out=bank[:],
+                    lhsT=w_codes[:, cols].bitcast(FP8X4),
+                    lhsT_scale=w_scales[:, cols],
+                    rhs=codes[:].bitcast(FP8X4),
+                    rhs_scale=scales[:],
+                    start=(j == 0),
+                    stop=(j == D_PASSES - 1),
+                )
+            col = fmap * CHUNKS + c
+            if g == 0:
+                features[fmap, c] = new_wide(F32, N)
+            nc.scalar.activation(
+                out=features[fmap, c][:].rearrange("p (u m) -> p u m", u=2)[:, :, g * HALF : (g + 1) * HALF],
+                in_=bank[:].rearrange("p (u m) -> p u m", u=2),
+                func=ACT.Tanh,
+                bias=bias[:, col : col + 1],
+                accum_out=sums[:, col * GROUPS + g : col * GROUPS + g + 1],
+            )
+
+        def feature_group(fmap, g):
+            for c in range(CHUNKS):
+                feature_chunk(fmap, g, c)
+
+        def mean(fmap, c):
+            col = fmap * CHUNKS + c
+            parts = sums[:, col * GROUPS : (col + 1) * GROUPS]
+            nc.scalar.activation(out=parts, in_=parts, func=ACT.Copy, scale=1.0 / N, accum_out=means[:, col : col + 1])
+
+        def last_feature_group(fmap):
+            for c in range(CHUNKS):
+                feature_chunk(fmap, GROUPS - 1, c)
+                if c > 0:
+                    mean(fmap, c - 1)
+            mean(fmap, CHUNKS - 1)
+
+        weighted, weighted_words, weighted_mx, moment_banks = {}, {}, {}, {}
+
+        def weigh(fmap, c, groups):
+            col = fmap * CHUNKS + c
+            if groups[0] == 0:
+                weighted[fmap, c] = work.tile([P, N], BF16, name="values", bufs=5, align_bytes=64)
+            span = slice(groups[0] * HALF, (groups[-1] + 1) * HALF)
+            nc.vector.scalar_tensor_tensor(
+                out=weighted[fmap, c][:].rearrange("p (u m) -> p u m", u=2)[:, :, span],
+                in0=features[fmap, c][:].rearrange("p (u m) -> p u m", u=2)[:, :, span],
+                scalar=means[:, col : col + 1],
+                in1=row_weight[fmap][:].rearrange("p (m u) -> p u m", u=2)[:, :, span],
+                op0=ALU.subtract,
+                op1=ALU.mult,
+            )
+
+        def turn_weighted(fmap, c, groups):
+            source = weighted[fmap, c][:].bitcast(F32)
+            if groups[0] == 0:
+                weighted_words[fmap, c] = new_words("xy"[fmap], 4)
+            for first_group in groups[::2]:
+                count = min(2, groups[-1] + 1 - first_group)
+                bank = new_bank()
+                for s in range(count):
+                    for u in range(2):
+                        first = 512 * u + P * (first_group + s)
+                        nc.tensor.transpose(
+                            bank[:, (2 * s + u) * P : (2 * s + u + 1) * P], source[:, first : first + P], ident[:]
+                        )
+                target = weighted_words[fmap, c][:, first_group * HALF : (first_group + count) * HALF]
+                nc.scalar.copy(
+                    out=target.rearrange("p (s k u) -> p s k u", s=count, u=2),
+                    in_=bank[:, 0 : count * HALF].rearrange("p (s u k) -> p s k u", s=count, u=2),
+                )
+
+        def quantize_weighted(fmap, c, groups):
+            if groups[0] == 0:
+                weighted_mx[fmap, c] = new_codes("xy"[fmap], (4, 8)[fmap])
+            codes, scales = weighted_mx[fmap, c]
+            cols = slice(groups[0] * P, (groups[-1] + 1) * P)
+            values = weighted_words[fmap, c][:].bitcast(BF16)[:, groups[0] * PASS : (groups[-1] + 1) * PASS]
+            quantize(codes[:, cols], scales[:, cols], values)
+
+        def moment(c, groups):
+            g_codes, g_scales = weighted_mx[G_MAP, c]
+            if groups[0] == 0:
+                moment_banks[c] = [new_bank(), new_bank()]
+            for g in groups:
+                cols = slice(g * P, (g + 1) * P)
+                for i in range(CHUNKS):
+                    f_codes, f_scales = weighted_mx[F_MAP, i]
+                    nc.tensor.matmul_mx(
+                        out=moment_banks[c][i // 2][:, (i % 2) * P : (i % 2 + 1) * P],
+                        lhsT=f_codes[:, cols].bitcast(FP8X4),
+                        lhsT_scale=f_scales[:, cols],
+                        rhs=g_codes[:, cols].bitcast(FP8X4),
+                        rhs_scale=g_scales[:, cols],
+                        start=(g == 0 and i % 2 == 0),
+                        stop=(g == GROUPS - 1 and i % 2 == 1),
+                    )
+
+        def store(c, side, on_vector):
+            result = work.tile([P, 2 * P], F32, name="result_%d" % side, bufs=2, align_bytes=256)
+            bank = moment_banks[c][side][:, 0 : 2 * P]
+            if on_vector:
+                nc.vector.tensor_scalar(out=result[:], in0=bank, scalar1=1.0 / math.sqrt(N), scalar2=None, op0=ALU.mult)
+            else:
+                nc.scalar.activation(out=result[:], in_=bank, func=ACT.Copy, scale=1.0 / math.sqrt(N))
+            nc.sync.dma_start(
+                out=out[side * HALF : (side + 1) * HALF, c * P : (c + 1) * P].rearrange("(i q) k -> q i k", q=P),
+                in_=result[:].rearrange("q (i k) -> q i k", k=P),
+            )
+
+        every = range(GROUPS)
+        interleave_w(F_MAP, 0, nc.scalar.copy)
+        widen_y(0)
+        widen_y(1)
+        turn_rows(F_MAP, 0)
+        turn_rows(F_MAP, 1)
+        quantize_w(F_MAP, 0)
+        interleave_w(F_MAP, 1, nc.vector.tensor_copy)
+        quantize_rows(F_MAP, 0)
+        quantize_w(F_MAP, 1)
+        turn_rows(G_MAP, 0)
+        turn_rows(G_MAP, 1)
+        turn_rows(F_MAP, 2)
+        turn_rows(F_MAP, 3)
+        widen_y(2)
+        feature_group(F_MAP, 0)
+        quantize_rows(F_MAP, 1)
+        quantize_rows(G_MAP, 0)
+        widen_y(3)
+        turn_rows(G_MAP, 2)
+        turn_rows(F_MAP, 4)
+        turn_rows(F_MAP, 5)
+        feature_group(F_MAP, 1)
+        quantize_rows(F_MAP, 2)
+        widen_y(4)
+        turn_rows(G_MAP, 3)
+        turn_rows(F_MAP, 6)
+        turn_rows(F_MAP, 7)
+        interleave_w(G_MAP, 0, nc.vector.tensor_copy)
+        quantize_rows(G_MAP, 1)
+        widen_y(5)
+        feature_group(F_MAP, 2)
+        quantize_rows(F_MAP, 3)
+        quantize_w(G_MAP, 0)
+        interleave_w(G_MAP, 1, nc.vector.tensor_copy)
+        turn_rows(G_MAP, 4)
+        turn_rows(G_MAP, 5)
+        last_feature_group(F_MAP)
+        widen_y(6)
+        quantize_w(G_MAP, 1)
+        widen_y(7)
+        quantize_rows(G_MAP, 2)
+        feature_group(G_MAP, 0)
+        turn_rows(G_MAP, 6)
+        turn_rows(G_MAP, 7)
+        weigh(F_MAP, 0, every)
+        feature_group(G_MAP, 1)
+        quantize_rows(G_MAP, 3)
+        weigh(F_MAP, 1, every)
+        feature_group(G_MAP, 2)
+        weigh(F_MAP, 2, every)
+        last_feature_group(G_MAP)
+        weigh(F_MAP, 3, every)
+        for c in range(CHUNKS):
+            turn_weighted(F_MAP, c, every)
+        weigh(G_MAP, 0, every)
+        quantize_weighted(F_MAP, 0, every)
+        quantize_weighted(F_MAP, 1, every)
+        turn_weighted(G_MAP, 0, every)
+        weigh(G_MAP, 1, every)
+        quantize_weighted(F_MAP, 2, every)
+        quantize_weighted(F_MAP, 3, every)
+        quantize_weighted(G_MAP, 0, every)
+        turn_weighted(G_MAP, 1, every)
+        moment(0, every)
+        weigh(G_MAP, 2, every)
+        store(0, 0, False)
+        store(0, 1, False)
+        quantize_weighted(G_MAP, 1, every)
+        turn_weighted(G_MAP, 2, every)
+        moment(1, every)
+        weigh(G_MAP, 3, range(0, 2))
+        quantize_weighted(G_MAP, 2, every)
+        turn_weighted(G_MAP, 3, range(0, 2))
+        store(1, 0, False)
+        store(1, 1, False)
+        weigh(G_MAP, 3, range(2, 3))
+        moment(2, range(0, 2))
+        weigh(G_MAP, 3, range(3, 4))
+        turn_weighted(G_MAP, 3, range(2, 3))
+        turn_weighted(G_MAP, 3, range(3, 4))
+        moment(2, range(2, 4))
+        quantize_weighted(G_MAP, 3, range(0, 2))
+        moment(3, range(0, 2))
+        quantize_weighted(G_MAP, 3, range(2, 3))
+        moment(3, range(2, 3))
+        quantize_weighted(G_MAP, 3, range(3, 4))
+        store(2, 0, False)
+        store(2, 1, False)
+        moment(3, range(3, 4))
+        store(3, 0, True)
+        store(3, 1, False)

@@ -30,18 +30,21 @@ def tile_twolobeweightedkoopmancrossmoment_kernel(tc, x, y_bytes, y_scale, w0, w
     with ExitStack() as ctx:
         keep = ctx.enter_context(tc.tile_pool(name="keep", bufs=1))
         work = ctx.enter_context(tc.tile_pool(name="work", bufs=2))
-        psum = ctx.enter_context(tc.psum_pool(name="psum", bufs=8))
+        psum = ctx.enter_context(tc.psum_pool(name="psum", bufs=6))
         ctx.enter_context(tc.manual_schedule())
 
         def new_bank():
             return psum.tile([P, PASS], F32, name="bank")
 
-        def new_words(stream, bufs):
-            return work.tile([P, 1024], F32, name="words_" + stream, bufs=bufs, align_bytes=64)
+        def new_held_bank():
+            return psum.tile([P, PASS], F32, name="held_bank", bufs=2)
 
-        def new_codes(stream, bufs):
-            codes = work.tile([P, PASS], U32, name="codes_" + stream, bufs=bufs, align_bytes=64)
-            scales = work.tile([P, PASS], U8, name="scales_" + stream, bufs=bufs, align_bytes=64)
+        def new_words(stream, bufs, columns):
+            return work.tile([P, columns], F32, name="words_" + stream, bufs=bufs, align_bytes=64)
+
+        def new_codes(stream, bufs, columns):
+            codes = work.tile([P, columns], U32, name="codes_" + stream, bufs=bufs, align_bytes=64)
+            scales = work.tile([P, columns], U8, name="scales_" + stream, bufs=bufs, align_bytes=64)
             return codes, scales
 
         def new_wide(dtype, columns):
@@ -76,21 +79,22 @@ def tile_twolobeweightedkoopmancrossmoment_kernel(tc, x, y_bytes, y_scale, w0, w
             row_weight[fmap] = keep.tile([P, N], BF16, name="row_weight_%d" % fmap, align_bytes=256)
             nc.sync.dma_start(out=row_weight[fmap][:], in_=(p, a)[fmap].partition_broadcast(P))
 
-        nc.sync.dma_start(out=scale_cols[:], in_=y_scale.rearrange("o (q i) -> q (o i)", i=8))
+        nc.sync.dma_start(out=scale_cols[:].rearrange("q (j t) -> q j t", t=4), in_=y_scale.rearrange("o (j q t) -> q (o j) t", q=P, t=4))
         nc.sync.dma_start(out=bias_rows[:], in_=b.rearrange("l (c q) -> (l c) q", q=P))
-        load_y(0)
-        load_w(F_MAP, 0)
-        load_x(0)
-        load_y(1)
-        load_x(1)
-        load_w(F_MAP, 1)
-        for g in range(1, GROUPS):
-            load_x(2 * g)
-            load_y(g + 1)
-            load_x(2 * g + 1)
+        for h in range(2):
+            load_y(h)
+            load_x(h)
+        for j in range(D_PASSES):
+            load_w(F_MAP, j)
+            load_y(2 + j)
+        for h in range(2, 6):
+            load_x(h)
         load_w(G_MAP, 0)
-        load_y(5)
+        load_y(4)
         load_w(G_MAP, 1)
+        load_x(6)
+        load_y(5)
+        load_x(7)
         load_y(6)
         load_y(7)
         load_row_weight(F_MAP)
@@ -102,18 +106,17 @@ def tile_twolobeweightedkoopmancrossmoment_kernel(tc, x, y_bytes, y_scale, w0, w
         nc.gpsimd.memset(bias_square[:], 0.0)
         nc.scalar.activation(out=bias_square[0:8, :], in_=bias_rows[:], func=ACT.Copy)
 
-        scale_rows = keep.tile([P, D], F32)
+        scale_rows = []
         for v in range(2):
-            bank = new_bank()
+            bank = new_held_bank()
+            scale_rows.append(bank)
             for i in range(4):
-                col = 4 * (i // 2) + 2 * v + i % 2
+                col = 4 * v + i
                 nc.tensor.transpose(
-                    bank[:, i * P : (i + 1) * P], scale_cols[:, col : col + 1].to_broadcast([P, P]), ident[:]
+                    bank[:].rearrange("p (q i) -> p q i", i=4)[:, :, i],
+                    scale_cols[:, col : col + 1].to_broadcast([P, P]),
+                    ident[:],
                 )
-            (nc.vector.tensor_copy, nc.scalar.copy)[v](
-                out=scale_rows[:, v * PASS : (v + 1) * PASS].rearrange("p (q i) -> p q i", i=4),
-                in_=bank[:].rearrange("p (i q) -> p q i", i=4),
-            )
 
         bias = keep.tile([P, 8], F32)
         bank = new_bank()
@@ -122,77 +125,78 @@ def tile_twolobeweightedkoopmancrossmoment_kernel(tc, x, y_bytes, y_scale, w0, w
 
         w_words, w_mx = {}, {}
 
-        def interleave_w(fmap, j, copy):
-            w_words[fmap, j] = new_words("w", 2)
-            copy(
-                out=w_words[fmap, j][:].bitcast(BF16).rearrange("p (k t) -> p k t", t=4),
-                in_=w_rows[fmap, j][:].rearrange("p (t k) -> p k t", t=4),
-            )
+        def interleave_w(fmap):
+            w_words[fmap] = new_words("shared", 1, 2048)
+            for j in range(D_PASSES):
+                nc.gpsimd.tensor_scalar(
+                    out=w_words[fmap][:, j * 1024 : (j + 1) * 1024].bitcast(BF16).rearrange("p (k t) -> p k t", t=4),
+                    in0=w_rows[fmap, j][:].rearrange("p (t k) -> p k t", t=4),
+                    scalar1=1.0,
+                    scalar2=0.0,
+                    op0=ALU.mult,
+                    op1=ALU.add,
+                )
 
-        def quantize_w(fmap, j):
-            codes = keep.tile([P, K], U32, name="w_codes_%d_%d" % (fmap, j), align_bytes=64)
-            scales = keep.tile([P, K], U8, name="w_scales_%d_%d" % (fmap, j), align_bytes=64)
-            quantize(codes[:], scales[:], w_words[fmap, j][:].bitcast(BF16))
-            w_mx[fmap, j] = (codes, scales)
+        def quantize_w(fmap):
+            codes = keep.tile([P, D_PASSES * K], U32, name="w_codes_%d" % fmap, align_bytes=64)
+            scales = keep.tile([P, D_PASSES * K], U8, name="w_scales_%d" % fmap, align_bytes=64)
+            quantize(codes[:], scales[:], w_words[fmap][:].bitcast(BF16))
+            w_mx[fmap] = (codes, scales)
 
         y_values = {}
 
         def widen_y(h):
             y_values[h] = work.tile([P, 2 * D], BF16, name="values", bufs=5, align_bytes=64)
             for u in range(2):
-                cols = slice(u * D, (u + 1) * D)
-                nc.vector.tensor_tensor(
-                    out=y_values[h][:, cols].rearrange("p (v m e) -> p v m e", v=2, e=2),
-                    in0=y_rows[h][:, cols].bitcast(FP8).rearrange("p (m v e) -> p v m e", v=2, e=2),
-                    in1=scale_rows[:].rearrange("p (v m e) -> p v m e", v=2, e=2),
-                    op=ALU.mult,
-                )
+                for j in range(D_PASSES):
+                    cols = slice(u * D + j * PASS, u * D + (j + 1) * PASS)
+                    nc.vector.tensor_tensor(
+                        out=y_values[h][:, cols], in0=y_rows[h][:, cols].bitcast(FP8), in1=scale_rows[j][:], op=ALU.mult
+                    )
 
         row_words = {}
 
         def turn_rows(fmap, h):
             g, side = divmod(h, 2)
             source = (x_rows, y_values)[fmap][h][:].bitcast(F32)
+            if side == 0:
+                if (fmap, g) == (F_MAP, 2):
+                    row_words[fmap, g] = new_words("shared", 1, 2048)
+                else:
+                    row_words[fmap, g] = new_words("xy"[fmap], 2, 2048)
             for j in range(D_PASSES):
-                if side == 0:
-                    row_words[fmap, g, j] = new_words("xy"[fmap], 4)
                 bank = new_bank()
                 for u in range(2):
                     for v in range(2):
-                        if fmap == F_MAP:
-                            first = 512 * u + 256 * j + v
-                            pairs = source[:, first : 512 * u + 256 * (j + 1) : 2]
-                        else:
-                            first = 512 * u + 256 * v + P * j
-                            pairs = source[:, first : first + P]
+                        pairs = source[:, 512 * u + 256 * j + v : 512 * u + 256 * (j + 1) : 2]
                         nc.tensor.transpose(bank[:, (2 * u + v) * P : (2 * u + v + 1) * P], pairs, ident[:])
-                target = row_words[fmap, g, j][:].rearrange("p (u s r v) -> p u s r v", u=2, s=2, v=2)
-                nc.scalar.copy(out=target[:, :, side, :, :], in_=bank[:].rearrange("p (u v r) -> p u r v", u=2, v=2))
+                target = row_words[fmap, g][:].rearrange("p (j u s r v) -> p j s u r v", j=2, u=2, s=2, v=2)
+                nc.scalar.copy(out=target[:, j, side, :, :, :], in_=bank[:].rearrange("p (u v r) -> p u r v", u=2, v=2))
 
         row_mx = {}
 
         def quantize_rows(fmap, g):
-            for j in range(D_PASSES):
-                row_mx[fmap, g, j] = new_codes("xy"[fmap], (4, 8)[fmap])
-                codes, scales = row_mx[fmap, g, j]
-                quantize(codes[:], scales[:], row_words[fmap, g, j][:].bitcast(BF16))
+            row_mx[fmap, g] = new_codes("xy"[fmap], (4, 4)[fmap], D_PASSES * PASS)
+            codes, scales = row_mx[fmap, g]
+            quantize(codes[:], scales[:], row_words[fmap, g][:].bitcast(BF16))
 
         features = {}
         sums = keep.tile([P, 2 * CHUNKS * GROUPS], F32)
         means = keep.tile([P, 2 * CHUNKS], F32)
 
         def feature_chunk(fmap, g, c):
-            cols = slice(c * P, (c + 1) * P)
             bank = new_bank()
+            w_codes, w_scales = w_mx[fmap]
+            codes, scales = row_mx[fmap, g]
             for j in range(D_PASSES):
-                w_codes, w_scales = w_mx[fmap, j]
-                codes, scales = row_mx[fmap, g, j]
+                cols = slice(j * K + c * P, j * K + (c + 1) * P)
+                rows = slice(j * PASS, (j + 1) * PASS)
                 nc.tensor.matmul_mx(
                     out=bank[:],
                     lhsT=w_codes[:, cols].bitcast(FP8X4),
                     lhsT_scale=w_scales[:, cols],
-                    rhs=codes[:].bitcast(FP8X4),
-                    rhs_scale=scales[:],
+                    rhs=codes[:, rows].bitcast(FP8X4),
+                    rhs_scale=scales[:, rows],
                     start=(j == 0),
                     stop=(j == D_PASSES - 1),
                 )
@@ -242,7 +246,10 @@ def tile_twolobeweightedkoopmancrossmoment_kernel(tc, x, y_bytes, y_scale, w0, w
         def turn_weighted(fmap, c, groups):
             source = weighted[fmap, c][:].bitcast(F32)
             if groups[0] == 0:
-                weighted_words[fmap, c] = new_words("xy"[fmap], 4)
+                if c % 2 == 0:
+                    both = new_words("xy"[fmap], 2, 2048)
+                    weighted_words[fmap, c] = both[:, 0:1024]
+                    weighted_words[fmap, c + 1] = both[:, 1024:2048]
             for first_group in groups[::2]:
                 count = min(2, groups[-1] + 1 - first_group)
                 bank = new_bank()
@@ -260,131 +267,128 @@ def tile_twolobeweightedkoopmancrossmoment_kernel(tc, x, y_bytes, y_scale, w0, w
 
         def quantize_weighted(fmap, c, groups):
             if groups[0] == 0:
-                weighted_mx[fmap, c] = new_codes("xy"[fmap], (4, 8)[fmap])
+                weighted_mx[fmap, c] = new_codes("xy"[fmap], 4, PASS)
             codes, scales = weighted_mx[fmap, c]
             cols = slice(groups[0] * P, (groups[-1] + 1) * P)
             values = weighted_words[fmap, c][:].bitcast(BF16)[:, groups[0] * PASS : (groups[-1] + 1) * PASS]
             quantize(codes[:, cols], scales[:, cols], values)
 
-        def moment(c, groups):
+        passes_done = {}
+
+        def moment(f_chunks, c, groups):
             g_codes, g_scales = weighted_mx[G_MAP, c]
-            if groups[0] == 0:
-                moment_banks[c] = [new_bank(), new_bank()]
             for g in groups:
                 cols = slice(g * P, (g + 1) * P)
-                for i in range(CHUNKS):
+                for i in f_chunks:
+                    blocks = 2 if c == CHUNKS - 1 else CHUNKS
+                    key = (c, i // blocks)
+                    if key not in moment_banks:
+                        moment_banks[key] = new_held_bank() if c < 2 else new_bank()
+                        passes_done[key] = 0
                     f_codes, f_scales = weighted_mx[F_MAP, i]
                     nc.tensor.matmul_mx(
-                        out=moment_banks[c][i // 2][:, (i % 2) * P : (i % 2 + 1) * P],
+                        out=moment_banks[key][:, (i % blocks) * P : (i % blocks + 1) * P],
                         lhsT=f_codes[:, cols].bitcast(FP8X4),
                         lhsT_scale=f_scales[:, cols],
                         rhs=g_codes[:, cols].bitcast(FP8X4),
                         rhs_scale=g_scales[:, cols],
-                        start=(g == 0 and i % 2 == 0),
-                        stop=(g == GROUPS - 1 and i % 2 == 1),
+                        start=(passes_done[key] == 0),
+                        stop=(passes_done[key] == blocks * GROUPS - 1),
                     )
+                    passes_done[key] += 1
 
         def store(c, side, on_vector):
-            result = work.tile([P, 2 * P], F32, name="result_%d" % side, bufs=2, align_bytes=256)
-            bank = moment_banks[c][side][:, 0 : 2 * P]
+            blocks = 2 if c == CHUNKS - 1 else CHUNKS
+            result = work.tile([P, blocks * P], F32, name="values", bufs=5, align_bytes=64)
+            bank = moment_banks[c, side][:, 0 : blocks * P]
             if on_vector:
                 nc.vector.tensor_scalar(out=result[:], in0=bank, scalar1=1.0 / math.sqrt(N), scalar2=None, op0=ALU.mult)
             else:
                 nc.scalar.activation(out=result[:], in_=bank, func=ACT.Copy, scale=1.0 / math.sqrt(N))
+            rows = slice(side * blocks * P, (side + 1) * blocks * P)
             nc.sync.dma_start(
-                out=out[side * HALF : (side + 1) * HALF, c * P : (c + 1) * P].rearrange("(i q) k -> q i k", q=P),
+                out=out[rows, c * P : (c + 1) * P].rearrange("(i q) k -> q i k", q=P),
                 in_=result[:].rearrange("q (i k) -> q i k", k=P),
             )
 
         every = range(GROUPS)
-        interleave_w(F_MAP, 0, nc.scalar.copy)
         widen_y(0)
-        widen_y(1)
         turn_rows(F_MAP, 0)
         turn_rows(F_MAP, 1)
-        quantize_w(F_MAP, 0)
-        interleave_w(F_MAP, 1, nc.vector.tensor_copy)
-        quantize_rows(F_MAP, 0)
-        quantize_w(F_MAP, 1)
+        interleave_w(F_MAP)
+        widen_y(1)
         turn_rows(G_MAP, 0)
         turn_rows(G_MAP, 1)
+        widen_y(2)
+        turn_rows(G_MAP, 2)
         turn_rows(F_MAP, 2)
         turn_rows(F_MAP, 3)
-        widen_y(2)
-        feature_group(F_MAP, 0)
+        widen_y(3)
+        turn_rows(G_MAP, 3)
+        quantize_rows(F_MAP, 0)
+        quantize_w(F_MAP)
         quantize_rows(F_MAP, 1)
         quantize_rows(G_MAP, 0)
-        widen_y(3)
-        turn_rows(G_MAP, 2)
         turn_rows(F_MAP, 4)
         turn_rows(F_MAP, 5)
-        feature_group(F_MAP, 1)
         quantize_rows(F_MAP, 2)
+        interleave_w(G_MAP)
+        feature_group(F_MAP, 0)
         widen_y(4)
-        turn_rows(G_MAP, 3)
         turn_rows(F_MAP, 6)
         turn_rows(F_MAP, 7)
-        interleave_w(G_MAP, 0, nc.vector.tensor_copy)
-        quantize_rows(G_MAP, 1)
         widen_y(5)
+        feature_group(F_MAP, 1)
+        widen_y(6)
         feature_group(F_MAP, 2)
         quantize_rows(F_MAP, 3)
-        quantize_w(G_MAP, 0)
-        interleave_w(G_MAP, 1, nc.vector.tensor_copy)
+        quantize_w(G_MAP)
+        quantize_rows(G_MAP, 1)
+        last_feature_group(F_MAP)
+        widen_y(7)
         turn_rows(G_MAP, 4)
         turn_rows(G_MAP, 5)
-        last_feature_group(F_MAP)
-        widen_y(6)
-        quantize_w(G_MAP, 1)
-        widen_y(7)
+        weigh(F_MAP, 0, every)
         quantize_rows(G_MAP, 2)
         feature_group(G_MAP, 0)
         turn_rows(G_MAP, 6)
         turn_rows(G_MAP, 7)
-        weigh(F_MAP, 0, every)
-        feature_group(G_MAP, 1)
-        quantize_rows(G_MAP, 3)
         weigh(F_MAP, 1, every)
-        feature_group(G_MAP, 2)
+        feature_group(G_MAP, 1)
         weigh(F_MAP, 2, every)
-        last_feature_group(G_MAP)
+        quantize_rows(G_MAP, 3)
         weigh(F_MAP, 3, every)
         for c in range(CHUNKS):
-            turn_weighted(F_MAP, c, every)
-        weigh(G_MAP, 0, every)
-        quantize_weighted(F_MAP, 0, every)
-        quantize_weighted(F_MAP, 1, every)
-        turn_weighted(G_MAP, 0, every)
-        weigh(G_MAP, 1, every)
-        quantize_weighted(F_MAP, 2, every)
-        quantize_weighted(F_MAP, 3, every)
-        quantize_weighted(G_MAP, 0, every)
-        turn_weighted(G_MAP, 1, every)
-        moment(0, every)
-        weigh(G_MAP, 2, every)
-        store(0, 0, False)
-        store(0, 1, False)
-        quantize_weighted(G_MAP, 1, every)
-        turn_weighted(G_MAP, 2, every)
-        moment(1, every)
-        weigh(G_MAP, 3, range(0, 2))
-        quantize_weighted(G_MAP, 2, every)
+            feature_chunk(G_MAP, 2, c)
+            feature_chunk(G_MAP, 3, c)
+            turn_weighted(F_MAP, c, range(0, 2))
+            mean(G_MAP, c)
+            turn_weighted(F_MAP, c, range(2, 4))
+            if c > 0:
+                turn_weighted(G_MAP, c - 1, every)
+            if c == 2:
+                moment(range(0, 2), 0, every)
+            if c == 3:
+                moment(range(2, 3), 0, every)
+                moment(range(0, 3), 1, every)
+                weigh(G_MAP, c, range(0, 2))
+            else:
+                weigh(G_MAP, c, every)
+            quantize_weighted(F_MAP, c, every)
+            if c > 0:
+                quantize_weighted(G_MAP, c - 1, every)
         turn_weighted(G_MAP, 3, range(0, 2))
-        store(1, 0, False)
-        store(1, 1, False)
-        weigh(G_MAP, 3, range(2, 3))
-        moment(2, range(0, 2))
-        weigh(G_MAP, 3, range(3, 4))
-        turn_weighted(G_MAP, 3, range(2, 3))
-        turn_weighted(G_MAP, 3, range(3, 4))
-        moment(2, range(2, 4))
+        moment(range(3, 4), 0, every)
+        moment(range(3, 4), 1, every)
+        weigh(G_MAP, 3, range(2, 4))
+        store(0, 0, False)
+        moment(range(0, 4), 2, range(0, 2))
+        turn_weighted(G_MAP, 3, range(2, 4))
         quantize_weighted(G_MAP, 3, range(0, 2))
-        moment(3, range(0, 2))
-        quantize_weighted(G_MAP, 3, range(2, 3))
-        moment(3, range(2, 3))
-        quantize_weighted(G_MAP, 3, range(3, 4))
+        moment(range(0, 4), 2, range(2, 4))
+        store(1, 0, True)
+        quantize_weighted(G_MAP, 3, range(2, 4))
+        moment(range(0, 4), 3, every)
         store(2, 0, False)
-        store(2, 1, False)
-        moment(3, range(3, 4))
         store(3, 0, True)
         store(3, 1, False)

@@ -80,13 +80,15 @@ def tile_twolobeweightedkoopmancrossmoment_kernel(tc, x, y_bytes, y_scale, w0, w
             nc.sync.dma_start(out=row_weight[fmap][:], in_=(p, a)[fmap].partition_broadcast(P))
 
         nc.sync.dma_start(out=scale_cols[:].rearrange("q (j t) -> q j t", t=4), in_=y_scale.rearrange("o (j q t) -> q (o j) t", q=P, t=4))
+        load_y(0)
         nc.sync.dma_start(out=bias_rows[:], in_=b.rearrange("l (c q) -> (l c) q", q=P))
-        for h in range(2):
-            load_y(h)
-            load_x(h)
-        for j in range(D_PASSES):
-            load_w(F_MAP, j)
-            load_y(2 + j)
+        load_x(0)
+        load_y(1)
+        load_w(F_MAP, 0)
+        load_x(1)
+        load_y(2)
+        load_w(F_MAP, 1)
+        load_y(3)
         for h in range(2, 6):
             load_x(h)
         load_w(G_MAP, 0)
@@ -97,6 +99,10 @@ def tile_twolobeweightedkoopmancrossmoment_kernel(tc, x, y_bytes, y_scale, w0, w
         load_x(7)
         load_y(6)
         load_y(7)
+        p_cols = keep.tile([P, 8], F32)
+        nc.sync.dma_start(
+            out=p_cols[:].rearrange("q (j t) -> q j t", t=4), in_=p.bitcast(F32).rearrange("(j q t) -> q j t", q=P, t=4)
+        )
         load_row_weight(F_MAP)
         load_row_weight(G_MAP)
 
@@ -106,17 +112,17 @@ def tile_twolobeweightedkoopmancrossmoment_kernel(tc, x, y_bytes, y_scale, w0, w
         nc.gpsimd.memset(bias_square[:], 0.0)
         nc.scalar.activation(out=bias_square[0:8, :], in_=bias_rows[:], func=ACT.Copy)
 
-        scale_rows = []
-        for v in range(2):
+        def spread(columns, j):
             bank = new_held_bank()
-            scale_rows.append(bank)
             for i in range(4):
-                col = 4 * v + i
                 nc.tensor.transpose(
                     bank[:].rearrange("p (q i) -> p q i", i=4)[:, :, i],
-                    scale_cols[:, col : col + 1].to_broadcast([P, P]),
+                    columns[:, 4 * j + i : 4 * j + i + 1].to_broadcast([P, P]),
                     ident[:],
                 )
+            return bank
+
+        scale_rows = [spread(scale_cols, j) for j in range(2)]
 
         bias = keep.tile([P, 8], F32)
         bank = new_bank()
@@ -146,9 +152,9 @@ def tile_twolobeweightedkoopmancrossmoment_kernel(tc, x, y_bytes, y_scale, w0, w
         y_values = {}
 
         def widen_y(h):
-            y_values[h] = work.tile([P, 2 * D], BF16, name="values", bufs=5, align_bytes=64)
-            for u in range(2):
-                for j in range(D_PASSES):
+            y_values[h] = work.tile([P, 2 * D], BF16, name="values", bufs=6, align_bytes=64)
+            for j in range(D_PASSES):
+                for u in range(2):
                     cols = slice(u * D + j * PASS, u * D + (j + 1) * PASS)
                     nc.vector.tensor_tensor(
                         out=y_values[h][:, cols], in0=y_rows[h][:, cols].bitcast(FP8), in1=scale_rows[j][:], op=ALU.mult
@@ -176,7 +182,7 @@ def tile_twolobeweightedkoopmancrossmoment_kernel(tc, x, y_bytes, y_scale, w0, w
         row_mx = {}
 
         def quantize_rows(fmap, g):
-            row_mx[fmap, g] = new_codes("xy"[fmap], (4, 4)[fmap], D_PASSES * PASS)
+            row_mx[fmap, g] = new_codes("xy"[fmap], (3, 4)[fmap], D_PASSES * PASS)
             codes, scales = row_mx[fmap, g]
             quantize(codes[:], scales[:], row_words[fmap, g][:].bitcast(BF16))
 
@@ -218,7 +224,7 @@ def tile_twolobeweightedkoopmancrossmoment_kernel(tc, x, y_bytes, y_scale, w0, w
         def mean(fmap, c):
             col = fmap * CHUNKS + c
             parts = sums[:, col * GROUPS : (col + 1) * GROUPS]
-            nc.scalar.activation(out=parts, in_=parts, func=ACT.Copy, scale=1.0 / N, accum_out=means[:, col : col + 1])
+            nc.scalar.activation(out=parts, in_=parts, func=ACT.Copy, scale=-1.0 / N, accum_out=means[:, col : col + 1])
 
         def last_feature_group(fmap):
             for c in range(CHUNKS):
@@ -229,18 +235,57 @@ def tile_twolobeweightedkoopmancrossmoment_kernel(tc, x, y_bytes, y_scale, w0, w
 
         weighted, weighted_words, weighted_mx, moment_banks = {}, {}, {}, {}
 
-        def weigh(fmap, c, groups):
+        def by_parity(tile, groups):
+            return tile[:].rearrange("p (u m) -> p u m", u=2)[:, :, groups[0] * HALF : (groups[-1] + 1) * HALF]
+
+        def new_weighted(fmap, c):
+            weighted[fmap, c] = work.tile([P, N], BF16, name="values", bufs=6, align_bytes=64)
+
+        def weigh(fmap, c, groups, weights):
             col = fmap * CHUNKS + c
-            if groups[0] == 0:
-                weighted[fmap, c] = work.tile([P, N], BF16, name="values", bufs=5, align_bytes=64)
-            span = slice(groups[0] * HALF, (groups[-1] + 1) * HALF)
             nc.vector.scalar_tensor_tensor(
-                out=weighted[fmap, c][:].rearrange("p (u m) -> p u m", u=2)[:, :, span],
-                in0=features[fmap, c][:].rearrange("p (u m) -> p u m", u=2)[:, :, span],
+                out=by_parity(weighted[fmap, c], groups),
+                in0=by_parity(features[fmap, c], groups),
                 scalar=means[:, col : col + 1],
-                in1=row_weight[fmap][:].rearrange("p (m u) -> p u m", u=2)[:, :, span],
-                op0=ALU.subtract,
+                in1=weights,
+                op0=ALU.add,
                 op1=ALU.mult,
+            )
+
+        def sbuf_weights(fmap, groups):
+            span = slice(groups[0] * HALF, (groups[-1] + 1) * HALF)
+            return row_weight[fmap][:].rearrange("p (m u) -> p u m", u=2)[:, :, span]
+
+        def weigh_g(c, groups):
+            if groups[0] == 0:
+                new_weighted(G_MAP, c)
+            weigh(G_MAP, c, groups, sbuf_weights(G_MAP, groups))
+
+        def weigh_f(c, groups):
+            if groups[0] == 0:
+                new_weighted(F_MAP, c)
+            for j in range(2):
+                part = [g for g in groups if g // 2 == j]
+                if part:
+                    span = slice(part[0] % 2 * HALF, (part[-1] % 2 + 1) * HALF)
+                    weigh(F_MAP, c, part, p_rows[j][:].bitcast(BF16).rearrange("p (m u) -> p u m", u=2)[:, :, span])
+
+        def weigh_f_on_gpsimd(c, groups):
+            new_weighted(F_MAP, c)
+            centred = new_words("shared", 1, N)
+            nc.gpsimd.tensor_scalar(
+                out=by_parity(centred, groups),
+                in0=by_parity(features[F_MAP, c], groups),
+                scalar1=means[:, c : c + 1],
+                scalar2=1.0,
+                op0=ALU.add,
+                op1=ALU.mult,
+            )
+            nc.gpsimd.tensor_tensor(
+                out=by_parity(weighted[F_MAP, c], groups),
+                in0=by_parity(centred, groups),
+                in1=sbuf_weights(F_MAP, groups),
+                op=ALU.mult,
             )
 
         def turn_weighted(fmap, c, groups):
@@ -266,8 +311,10 @@ def tile_twolobeweightedkoopmancrossmoment_kernel(tc, x, y_bytes, y_scale, w0, w
                 )
 
         def quantize_weighted(fmap, c, groups):
-            if groups[0] == 0:
-                weighted_mx[fmap, c] = new_codes("xy"[fmap], 4, PASS)
+            if groups[0] == 0 and c % 2 == 0:
+                pair = new_codes("xy"[fmap], (3, 4)[fmap], 2 * PASS)
+                weighted_mx[fmap, c] = [part[:, 0:PASS] for part in pair]
+                weighted_mx[fmap, c + 1] = [part[:, PASS : 2 * PASS] for part in pair]
             codes, scales = weighted_mx[fmap, c]
             cols = slice(groups[0] * P, (groups[-1] + 1) * P)
             values = weighted_words[fmap, c][:].bitcast(BF16)[:, groups[0] * PASS : (groups[-1] + 1) * PASS]
@@ -299,7 +346,7 @@ def tile_twolobeweightedkoopmancrossmoment_kernel(tc, x, y_bytes, y_scale, w0, w
 
         def store(c, side, on_vector):
             blocks = 2 if c == CHUNKS - 1 else CHUNKS
-            result = work.tile([P, blocks * P], F32, name="values", bufs=5, align_bytes=64)
+            result = work.tile([P, blocks * P], F32, name="values", bufs=6, align_bytes=64)
             bank = moment_banks[c, side][:, 0 : blocks * P]
             if on_vector:
                 nc.vector.tensor_scalar(out=result[:], in0=bank, scalar1=1.0 / math.sqrt(N), scalar2=None, op0=ALU.mult)
@@ -314,10 +361,10 @@ def tile_twolobeweightedkoopmancrossmoment_kernel(tc, x, y_bytes, y_scale, w0, w
         every = range(GROUPS)
         widen_y(0)
         turn_rows(F_MAP, 0)
-        turn_rows(F_MAP, 1)
+        turn_rows(G_MAP, 0)
         interleave_w(F_MAP)
         widen_y(1)
-        turn_rows(G_MAP, 0)
+        turn_rows(F_MAP, 1)
         turn_rows(G_MAP, 1)
         widen_y(2)
         turn_rows(G_MAP, 2)
@@ -340,24 +387,30 @@ def tile_twolobeweightedkoopmancrossmoment_kernel(tc, x, y_bytes, y_scale, w0, w
         widen_y(5)
         feature_group(F_MAP, 1)
         widen_y(6)
-        feature_group(F_MAP, 2)
         quantize_rows(F_MAP, 3)
-        quantize_w(G_MAP)
         quantize_rows(G_MAP, 1)
-        last_feature_group(F_MAP)
-        widen_y(7)
+        quantize_w(G_MAP)
+        feature_group(F_MAP, 2)
         turn_rows(G_MAP, 4)
+        last_feature_group(F_MAP)
+        weigh_f_on_gpsimd(0, range(0, 3))
         turn_rows(G_MAP, 5)
-        weigh(F_MAP, 0, every)
-        quantize_rows(G_MAP, 2)
-        feature_group(G_MAP, 0)
+        widen_y(7)
+        p_rows = [spread(p_cols, 0)]
         turn_rows(G_MAP, 6)
+        p_rows.append(spread(p_cols, 1))
+        weigh_f(1, every)
+        feature_chunk(G_MAP, 0, 0)
+        feature_chunk(G_MAP, 1, 0)
         turn_rows(G_MAP, 7)
-        weigh(F_MAP, 1, every)
-        feature_group(G_MAP, 1)
-        weigh(F_MAP, 2, every)
+        weigh_f(2, every)
+        quantize_rows(G_MAP, 2)
         quantize_rows(G_MAP, 3)
-        weigh(F_MAP, 3, every)
+        for c in range(1, CHUNKS):
+            feature_chunk(G_MAP, 0, c)
+            feature_chunk(G_MAP, 1, c)
+        weigh_f(0, range(3, 4))
+        weigh_f(3, every)
         for c in range(CHUNKS):
             feature_chunk(G_MAP, 2, c)
             feature_chunk(G_MAP, 3, c)
@@ -371,24 +424,27 @@ def tile_twolobeweightedkoopmancrossmoment_kernel(tc, x, y_bytes, y_scale, w0, w
             if c == 3:
                 moment(range(2, 3), 0, every)
                 moment(range(0, 3), 1, every)
-                weigh(G_MAP, c, range(0, 2))
+                weigh_g(c, range(0, 2))
             else:
-                weigh(G_MAP, c, every)
+                weigh_g(c, every)
             quantize_weighted(F_MAP, c, every)
             if c > 0:
                 quantize_weighted(G_MAP, c - 1, every)
         turn_weighted(G_MAP, 3, range(0, 2))
         moment(range(3, 4), 0, every)
         moment(range(3, 4), 1, every)
-        weigh(G_MAP, 3, range(2, 4))
+        weigh_g(3, range(2, 3))
+        weigh_g(3, range(3, 4))
         store(0, 0, False)
-        moment(range(0, 4), 2, range(0, 2))
-        turn_weighted(G_MAP, 3, range(2, 4))
+        moment(every, 2, range(0, 2))
+        turn_weighted(G_MAP, 3, range(2, 3))
+        turn_weighted(G_MAP, 3, range(3, 4))
         quantize_weighted(G_MAP, 3, range(0, 2))
-        moment(range(0, 4), 2, range(2, 4))
         store(1, 0, True)
-        quantize_weighted(G_MAP, 3, range(2, 4))
-        moment(range(0, 4), 3, every)
+        moment(every, 2, range(2, 4))
+        quantize_weighted(G_MAP, 3, range(2, 3))
+        quantize_weighted(G_MAP, 3, range(3, 4))
+        moment(every, 3, every)
         store(2, 0, False)
         store(3, 0, True)
         store(3, 1, False)

@@ -17,12 +17,23 @@ ALU = mybir.AluOpType
 ACT = mybir.ActivationFunctionType
 
 P = 128
-PASS = 512
-HALF = 256
+PACK = 4
+PASS = P * PACK
+HALF = PASS // 2
 D_PASSES = D // PASS
 GROUPS = N // PASS
 CHUNKS = K // P
+LAST = CHUNKS - 1
 F_MAP, G_MAP = 0, 1
+STREAM = ("x", "y")
+
+HELD_BANKS = 2
+TURNING_BANKS = 6
+STAGING_BUFS = 6
+PAIR_BUFS = 2
+CODE_BUFS = (3, 4)
+GPSIMD_GROUPS = range(0, 3)
+GPSIMD_ROWS = len(GPSIMD_GROUPS) * PASS
 
 
 def tile_twolobeweightedkoopmancrossmoment_kernel(tc, x, y_bytes, y_scale, w0, w1, b, p, a, out):
@@ -30,113 +41,121 @@ def tile_twolobeweightedkoopmancrossmoment_kernel(tc, x, y_bytes, y_scale, w0, w
     with ExitStack() as ctx:
         keep = ctx.enter_context(tc.tile_pool(name="keep", bufs=1))
         work = ctx.enter_context(tc.tile_pool(name="work", bufs=2))
-        psum = ctx.enter_context(tc.psum_pool(name="psum", bufs=6))
+        psum = ctx.enter_context(tc.psum_pool(name="psum", bufs=TURNING_BANKS))
         ctx.enter_context(tc.manual_schedule())
 
         def new_bank():
             return psum.tile([P, PASS], F32, name="bank")
 
         def new_held_bank():
-            return psum.tile([P, PASS], F32, name="held_bank", bufs=2)
+            return psum.tile([P, PASS], F32, name="held_bank", bufs=HELD_BANKS)
 
-        def new_words(stream, bufs, columns):
-            return work.tile([P, columns], F32, name="words_" + stream, bufs=bufs, align_bytes=64)
+        def new_staging(columns, dtype):
+            return work.tile([P, columns], dtype, name="staging", bufs=STAGING_BUFS, align_bytes=64)
 
-        def new_codes(stream, bufs, columns):
-            codes = work.tile([P, columns], U32, name="codes_" + stream, bufs=bufs, align_bytes=64)
-            scales = work.tile([P, columns], U8, name="scales_" + stream, bufs=bufs, align_bytes=64)
+        def new_pairs(fmap):
+            return work.tile([P, 2048], F32, name="pairs_" + STREAM[fmap], bufs=PAIR_BUFS, align_bytes=64)
+
+        def new_gpsimd_buffer():
+            return work.tile([P, 2048], F32, name="gpsimd_buffer", bufs=1, align_bytes=64)
+
+        def new_codes(fmap):
+            bufs = CODE_BUFS[fmap]
+            codes = work.tile([P, 2 * PASS], U32, name="codes_" + STREAM[fmap], bufs=bufs, align_bytes=64)
+            scales = work.tile([P, 2 * PASS], U8, name="scales_" + STREAM[fmap], bufs=bufs, align_bytes=64)
             return codes, scales
 
-        def new_wide(dtype, columns):
+        def new_wide(columns, dtype):
             return work.tile([P, columns], dtype, name="wide", bufs=2 * CHUNKS, align_bytes=256)
 
         def quantize(codes, scales, values):
             nc.vector.quantize_mx(out=codes.bitcast(FP8X4), scales=scales, in_=values)
 
-        scale_cols = keep.tile([P, 8], F32)
-        bias_rows = keep.tile([8, P], BF16)
         w_rows, x_rows, y_rows, row_weight = {}, {}, {}, {}
+
+        def load_columns(name, vector):
+            columns = keep.tile([P, 2 * PACK], F32, name=name)
+            nc.sync.dma_start(
+                out=columns[:].rearrange("q (j t) -> q j t", t=PACK),
+                in_=vector.rearrange("(j q t) -> q j t", q=P, t=PACK),
+            )
+            return columns
 
         def load_w(fmap, j):
             if j == 0:
-                both = new_wide(BF16, D_PASSES * 4 * K)
+                both_passes = new_wide(D_PASSES * PACK * K, BF16)
                 for i in range(D_PASSES):
-                    w_rows[fmap, i] = both[:, i * 4 * K : (i + 1) * 4 * K]
-            src = (w0, w1)[fmap][j * PASS : (j + 1) * PASS, :]
-            nc.sync.dma_start(out=w_rows[fmap, j][:], in_=src.rearrange("(p t) k -> p (t k)", t=4))
+                    w_rows[fmap, i] = both_passes[:, i * PACK * K : (i + 1) * PACK * K]
+            rows = (w0, w1)[fmap][j * PASS : (j + 1) * PASS, :]
+            nc.sync.dma_start(out=w_rows[fmap, j], in_=rows.rearrange("(q t) k -> q (t k)", t=PACK))
 
         def load_x(h):
             x_rows[h] = keep.tile([P, 2 * D], BF16, name="x_rows_%d" % h, align_bytes=256)
-            nc.sync.dma_start(out=x_rows[h][:], in_=x[h * HALF : (h + 1) * HALF, :].rearrange("(r u) d -> r (u d)", u=2))
+            rows = x[h * HALF : (h + 1) * HALF, :]
+            nc.sync.dma_start(out=x_rows[h][:], in_=rows.rearrange("(r u) d -> r (u d)", u=2))
 
         def load_y(h):
             y_rows[h] = keep.tile([P, 2 * D], U8, name="y_byte_rows_%d" % h, align_bytes=256)
-            nc.sync.dma_start(
-                out=y_rows[h][:], in_=y_bytes[h * HALF : (h + 1) * HALF, :].rearrange("(r u) d -> r (u d)", u=2)
-            )
+            rows = y_bytes[h * HALF : (h + 1) * HALF, :]
+            nc.sync.dma_start(out=y_rows[h][:], in_=rows.rearrange("(r u) d -> r (u d)", u=2))
 
-        def load_row_weight(fmap):
-            row_weight[fmap] = keep.tile([P, N], BF16, name="row_weight_%d" % fmap, align_bytes=256)
-            nc.sync.dma_start(out=row_weight[fmap][:], in_=(p, a)[fmap].partition_broadcast(P))
+        def load_row_weight(fmap, rows):
+            row_weight[fmap] = keep.tile([P, rows], BF16, name="row_weight_%d" % fmap, align_bytes=256)
+            nc.sync.dma_start(out=row_weight[fmap][:], in_=(p, a)[fmap][0:rows].partition_broadcast(P))
 
-        nc.sync.dma_start(out=scale_cols[:].rearrange("q (j t) -> q j t", t=4), in_=y_scale.rearrange("o (j q t) -> q (o j) t", q=P, t=4))
+        scale_columns = load_columns("scale_columns", y_scale.rearrange("o d -> (o d)"))
         load_y(0)
+        bias_rows = keep.tile([2 * CHUNKS, P], BF16)
         nc.sync.dma_start(out=bias_rows[:], in_=b.rearrange("l (c q) -> (l c) q", q=P))
-        load_x(0)
-        load_y(1)
-        load_w(F_MAP, 0)
-        load_x(1)
-        load_y(2)
-        load_w(F_MAP, 1)
+        for j in range(D_PASSES):
+            load_x(j)
+            load_y(j + 1)
+            load_w(F_MAP, j)
         load_y(3)
         for h in range(2, 6):
             load_x(h)
         load_w(G_MAP, 0)
         load_y(4)
         load_w(G_MAP, 1)
-        load_x(6)
-        load_y(5)
-        load_x(7)
-        load_y(6)
+        for h in range(6, 8):
+            load_x(h)
+            load_y(h - 1)
         load_y(7)
-        p_cols = keep.tile([P, 8], F32)
-        nc.sync.dma_start(
-            out=p_cols[:].rearrange("q (j t) -> q j t", t=4), in_=p.bitcast(F32).rearrange("(j q t) -> q j t", q=P, t=4)
-        )
-        load_row_weight(F_MAP)
-        load_row_weight(G_MAP)
+        p_columns = load_columns("p_columns", p.bitcast(F32))
+        load_row_weight(F_MAP, GPSIMD_ROWS)
+        load_row_weight(G_MAP, N)
 
         ident = keep.tile([P, P], F32)
         make_identity(nc, ident[:])
         bias_square = keep.tile([P, P], F32)
         nc.gpsimd.memset(bias_square[:], 0.0)
-        nc.scalar.activation(out=bias_square[0:8, :], in_=bias_rows[:], func=ACT.Copy)
+        nc.scalar.activation(out=bias_square[0 : 2 * CHUNKS, :], in_=bias_rows[:], func=ACT.Copy)
 
         def spread(columns, j):
             bank = new_held_bank()
-            for i in range(4):
+            for t in range(PACK):
                 nc.tensor.transpose(
-                    bank[:].rearrange("p (q i) -> p q i", i=4)[:, :, i],
-                    columns[:, 4 * j + i : 4 * j + i + 1].to_broadcast([P, P]),
+                    bank[:].rearrange("r (q t) -> r q t", t=PACK)[:, :, t],
+                    columns[:, PACK * j + t : PACK * j + t + 1].to_broadcast([P, P]),
                     ident[:],
                 )
             return bank
 
-        scale_rows = [spread(scale_cols, j) for j in range(2)]
+        scale_banks = [spread(scale_columns, j) for j in range(D_PASSES)]
 
-        bias = keep.tile([P, 8], F32)
-        bank = new_bank()
-        nc.tensor.transpose(bank[:, 0:P], bias_square[:], ident[:])
-        nc.scalar.copy(out=bias[:], in_=bank[:, 0:8])
+        bias = keep.tile([P, 2 * CHUNKS], F32)
+        bias_bank = new_bank()
+        nc.tensor.transpose(bias_bank[:, 0:P], bias_square[:], ident[:])
+        nc.scalar.copy(out=bias[:], in_=bias_bank[:, 0 : 2 * CHUNKS])
 
-        w_words, w_mx = {}, {}
+        w_values, w_mx, y_values, row_pairs, row_mx, features = {}, {}, {}, {}, {}, {}
 
         def interleave_w(fmap):
-            w_words[fmap] = new_words("shared", 1, 2048)
+            w_values[fmap] = new_gpsimd_buffer()[:].bitcast(BF16)
             for j in range(D_PASSES):
                 nc.gpsimd.tensor_scalar(
-                    out=w_words[fmap][:, j * 1024 : (j + 1) * 1024].bitcast(BF16).rearrange("p (k t) -> p k t", t=4),
-                    in0=w_rows[fmap, j][:].rearrange("p (t k) -> p k t", t=4),
+                    out=w_values[fmap][:, j * PACK * K : (j + 1) * PACK * K].rearrange("q (k t) -> q k t", t=PACK),
+                    in0=w_rows[fmap, j].rearrange("q (t k) -> q k t", t=PACK),
                     scalar1=1.0,
                     scalar2=0.0,
                     op0=ALU.mult,
@@ -146,137 +165,122 @@ def tile_twolobeweightedkoopmancrossmoment_kernel(tc, x, y_bytes, y_scale, w0, w
         def quantize_w(fmap):
             codes = keep.tile([P, D_PASSES * K], U32, name="w_codes_%d" % fmap, align_bytes=64)
             scales = keep.tile([P, D_PASSES * K], U8, name="w_scales_%d" % fmap, align_bytes=64)
-            quantize(codes[:], scales[:], w_words[fmap][:].bitcast(BF16))
+            quantize(codes[:], scales[:], w_values[fmap])
             w_mx[fmap] = (codes, scales)
 
-        y_values = {}
-
         def widen_y(h):
-            y_values[h] = work.tile([P, 2 * D], BF16, name="values", bufs=6, align_bytes=64)
+            y_values[h] = new_staging(2 * D, BF16)
             for j in range(D_PASSES):
                 for u in range(2):
                     cols = slice(u * D + j * PASS, u * D + (j + 1) * PASS)
                     nc.vector.tensor_tensor(
-                        out=y_values[h][:, cols], in0=y_rows[h][:, cols].bitcast(FP8), in1=scale_rows[j][:], op=ALU.mult
+                        out=y_values[h][:, cols],
+                        in0=y_rows[h][:, cols].bitcast(FP8),
+                        in1=scale_banks[j][:],
+                        op=ALU.mult,
                     )
-
-        row_words = {}
 
         def turn_rows(fmap, h):
             g, side = divmod(h, 2)
             source = (x_rows, y_values)[fmap][h][:].bitcast(F32)
             if side == 0:
-                if (fmap, g) == (F_MAP, 2):
-                    row_words[fmap, g] = new_words("shared", 1, 2048)
-                else:
-                    row_words[fmap, g] = new_words("xy"[fmap], 2, 2048)
+                row_pairs[fmap, g] = new_gpsimd_buffer() if (fmap, g) == (F_MAP, 2) else new_pairs(fmap)
+            target = row_pairs[fmap, g][:].rearrange("q (j u s r v) -> q j s u r v", j=D_PASSES, u=2, s=2, v=2)
             for j in range(D_PASSES):
                 bank = new_bank()
                 for u in range(2):
+                    first = u * (D // 2) + j * HALF
                     for v in range(2):
-                        pairs = source[:, 512 * u + 256 * j + v : 512 * u + 256 * (j + 1) : 2]
-                        nc.tensor.transpose(bank[:, (2 * u + v) * P : (2 * u + v + 1) * P], pairs, ident[:])
-                target = row_words[fmap, g][:].rearrange("p (j u s r v) -> p j s u r v", j=2, u=2, s=2, v=2)
-                nc.scalar.copy(out=target[:, j, side, :, :, :], in_=bank[:].rearrange("p (u v r) -> p u r v", u=2, v=2))
-
-        row_mx = {}
+                        nc.tensor.transpose(
+                            bank[:, (2 * u + v) * P : (2 * u + v + 1) * P],
+                            source[:, first + v : first + HALF : 2],
+                            ident[:],
+                        )
+                nc.scalar.copy(out=target[:, j, side, :, :, :], in_=bank[:].rearrange("q (u v r) -> q u r v", u=2, v=2))
 
         def quantize_rows(fmap, g):
-            row_mx[fmap, g] = new_codes("xy"[fmap], (3, 4)[fmap], D_PASSES * PASS)
+            row_mx[fmap, g] = new_codes(fmap)
             codes, scales = row_mx[fmap, g]
-            quantize(codes[:], scales[:], row_words[fmap, g][:].bitcast(BF16))
+            quantize(codes[:], scales[:], row_pairs[fmap, g][:].bitcast(BF16))
 
-        features = {}
-        sums = keep.tile([P, 2 * CHUNKS * GROUPS], F32)
-        means = keep.tile([P, 2 * CHUNKS], F32)
+        group_sums = keep.tile([P, 2 * CHUNKS * GROUPS], F32)
+        minus_mean = keep.tile([P, 2 * CHUNKS], F32)
+
+        def by_parity(tile, groups):
+            return tile[:].rearrange("q (u m) -> q u m", u=2)[:, :, groups[0] * HALF : (groups[-1] + 1) * HALF]
 
         def feature_chunk(fmap, g, c):
             bank = new_bank()
             w_codes, w_scales = w_mx[fmap]
-            codes, scales = row_mx[fmap, g]
+            row_codes, row_scales = row_mx[fmap, g]
             for j in range(D_PASSES):
-                cols = slice(j * K + c * P, j * K + (c + 1) * P)
-                rows = slice(j * PASS, (j + 1) * PASS)
+                w_cols = slice(j * K + c * P, j * K + (c + 1) * P)
+                row_cols = slice(j * PASS, (j + 1) * PASS)
                 nc.tensor.matmul_mx(
                     out=bank[:],
-                    lhsT=w_codes[:, cols].bitcast(FP8X4),
-                    lhsT_scale=w_scales[:, cols],
-                    rhs=codes[:, rows].bitcast(FP8X4),
-                    rhs_scale=scales[:, rows],
+                    lhsT=w_codes[:, w_cols].bitcast(FP8X4),
+                    lhsT_scale=w_scales[:, w_cols],
+                    rhs=row_codes[:, row_cols].bitcast(FP8X4),
+                    rhs_scale=row_scales[:, row_cols],
                     start=(j == 0),
                     stop=(j == D_PASSES - 1),
                 )
             col = fmap * CHUNKS + c
             if g == 0:
-                features[fmap, c] = new_wide(F32, N)
+                features[fmap, c] = new_wide(N, F32)
             nc.scalar.activation(
-                out=features[fmap, c][:].rearrange("p (u m) -> p u m", u=2)[:, :, g * HALF : (g + 1) * HALF],
-                in_=bank[:].rearrange("p (u m) -> p u m", u=2),
+                out=by_parity(features[fmap, c], [g]),
+                in_=bank[:].rearrange("q (u m) -> q u m", u=2),
                 func=ACT.Tanh,
                 bias=bias[:, col : col + 1],
-                accum_out=sums[:, col * GROUPS + g : col * GROUPS + g + 1],
+                accum_out=group_sums[:, col * GROUPS + g : col * GROUPS + g + 1],
             )
 
         def feature_group(fmap, g):
             for c in range(CHUNKS):
                 feature_chunk(fmap, g, c)
 
-        def mean(fmap, c):
+        def take_mean(fmap, c):
             col = fmap * CHUNKS + c
-            parts = sums[:, col * GROUPS : (col + 1) * GROUPS]
-            nc.scalar.activation(out=parts, in_=parts, func=ACT.Copy, scale=-1.0 / N, accum_out=means[:, col : col + 1])
+            parts = group_sums[:, col * GROUPS : (col + 1) * GROUPS]
+            nc.scalar.activation(
+                out=parts, in_=parts, func=ACT.Copy, scale=-1.0 / N, accum_out=minus_mean[:, col : col + 1]
+            )
 
-        def last_feature_group(fmap):
-            for c in range(CHUNKS):
-                feature_chunk(fmap, GROUPS - 1, c)
-                if c > 0:
-                    mean(fmap, c - 1)
-            mean(fmap, CHUNKS - 1)
+        weighted, weighted_pairs, weighted_mx, out_banks, passes_done = {}, {}, {}, {}, {}
 
-        weighted, weighted_words, weighted_mx, moment_banks = {}, {}, {}, {}
-
-        def by_parity(tile, groups):
-            return tile[:].rearrange("p (u m) -> p u m", u=2)[:, :, groups[0] * HALF : (groups[-1] + 1) * HALF]
-
-        def new_weighted(fmap, c):
-            weighted[fmap, c] = work.tile([P, N], BF16, name="values", bufs=6, align_bytes=64)
+        def weights_by_parity(weights, first_group, groups):
+            span = slice((groups[0] - first_group) * HALF, (groups[-1] + 1 - first_group) * HALF)
+            return weights.rearrange("q (m u) -> q u m", u=2)[:, :, span]
 
         def weigh(fmap, c, groups, weights):
+            if (fmap, c) not in weighted:
+                weighted[fmap, c] = new_staging(N, BF16)
             col = fmap * CHUNKS + c
             nc.vector.scalar_tensor_tensor(
                 out=by_parity(weighted[fmap, c], groups),
                 in0=by_parity(features[fmap, c], groups),
-                scalar=means[:, col : col + 1],
+                scalar=minus_mean[:, col : col + 1],
                 in1=weights,
                 op0=ALU.add,
                 op1=ALU.mult,
             )
 
-        def sbuf_weights(fmap, groups):
-            span = slice(groups[0] * HALF, (groups[-1] + 1) * HALF)
-            return row_weight[fmap][:].rearrange("p (m u) -> p u m", u=2)[:, :, span]
-
         def weigh_g(c, groups):
-            if groups[0] == 0:
-                new_weighted(G_MAP, c)
-            weigh(G_MAP, c, groups, sbuf_weights(G_MAP, groups))
+            weigh(G_MAP, c, groups, weights_by_parity(row_weight[G_MAP][:], 0, groups))
 
-        def weigh_f(c, groups):
-            if groups[0] == 0:
-                new_weighted(F_MAP, c)
-            for j in range(2):
+        def weigh_f(c, groups, p_banks):
+            for j in sorted(set(g // 2 for g in groups)):
                 part = [g for g in groups if g // 2 == j]
-                if part:
-                    span = slice(part[0] % 2 * HALF, (part[-1] % 2 + 1) * HALF)
-                    weigh(F_MAP, c, part, p_rows[j][:].bitcast(BF16).rearrange("p (m u) -> p u m", u=2)[:, :, span])
+                weigh(F_MAP, c, part, weights_by_parity(p_banks[j][:].bitcast(BF16), 2 * j, part))
 
         def weigh_f_on_gpsimd(c, groups):
-            new_weighted(F_MAP, c)
-            centred = new_words("shared", 1, N)
+            weighted[F_MAP, c] = new_staging(N, BF16)
+            centred = new_gpsimd_buffer()
             nc.gpsimd.tensor_scalar(
                 out=by_parity(centred, groups),
                 in0=by_parity(features[F_MAP, c], groups),
-                scalar1=means[:, c : c + 1],
+                scalar1=minus_mean[:, c : c + 1],
                 scalar2=1.0,
                 op0=ALU.add,
                 op1=ALU.mult,
@@ -284,57 +288,57 @@ def tile_twolobeweightedkoopmancrossmoment_kernel(tc, x, y_bytes, y_scale, w0, w
             nc.gpsimd.tensor_tensor(
                 out=by_parity(weighted[F_MAP, c], groups),
                 in0=by_parity(centred, groups),
-                in1=sbuf_weights(F_MAP, groups),
+                in1=weights_by_parity(row_weight[F_MAP][:], 0, groups),
                 op=ALU.mult,
             )
 
         def turn_weighted(fmap, c, groups):
             source = weighted[fmap, c][:].bitcast(F32)
-            if groups[0] == 0:
-                if c % 2 == 0:
-                    both = new_words("xy"[fmap], 2, 2048)
-                    weighted_words[fmap, c] = both[:, 0:1024]
-                    weighted_words[fmap, c + 1] = both[:, 1024:2048]
+            if (fmap, c) not in weighted_pairs:
+                two_chunks = new_pairs(fmap)
+                weighted_pairs[fmap, c] = two_chunks[:, 0 : N // 2]
+                weighted_pairs[fmap, c + 1] = two_chunks[:, N // 2 : N]
             for first_group in groups[::2]:
                 count = min(2, groups[-1] + 1 - first_group)
                 bank = new_bank()
                 for s in range(count):
                     for u in range(2):
-                        first = 512 * u + P * (first_group + s)
+                        first = u * (N // 4) + (first_group + s) * P
                         nc.tensor.transpose(
                             bank[:, (2 * s + u) * P : (2 * s + u + 1) * P], source[:, first : first + P], ident[:]
                         )
-                target = weighted_words[fmap, c][:, first_group * HALF : (first_group + count) * HALF]
+                target = weighted_pairs[fmap, c][:, first_group * HALF : (first_group + count) * HALF]
                 nc.scalar.copy(
-                    out=target.rearrange("p (s k u) -> p s k u", s=count, u=2),
-                    in_=bank[:, 0 : count * HALF].rearrange("p (s u k) -> p s k u", s=count, u=2),
+                    out=target.rearrange("q (s k u) -> q s k u", s=count, u=2),
+                    in_=bank[:, 0 : count * HALF].rearrange("q (s u k) -> q s k u", s=count, u=2),
                 )
 
         def quantize_weighted(fmap, c, groups):
-            if groups[0] == 0 and c % 2 == 0:
-                pair = new_codes("xy"[fmap], (3, 4)[fmap], 2 * PASS)
-                weighted_mx[fmap, c] = [part[:, 0:PASS] for part in pair]
-                weighted_mx[fmap, c + 1] = [part[:, PASS : 2 * PASS] for part in pair]
+            if (fmap, c) not in weighted_mx:
+                two_chunks = new_codes(fmap)
+                weighted_mx[fmap, c] = [part[:, 0:PASS] for part in two_chunks]
+                weighted_mx[fmap, c + 1] = [part[:, PASS : 2 * PASS] for part in two_chunks]
             codes, scales = weighted_mx[fmap, c]
             cols = slice(groups[0] * P, (groups[-1] + 1) * P)
-            values = weighted_words[fmap, c][:].bitcast(BF16)[:, groups[0] * PASS : (groups[-1] + 1) * PASS]
+            values = weighted_pairs[fmap, c].bitcast(BF16)[:, groups[0] * PASS : (groups[-1] + 1) * PASS]
             quantize(codes[:, cols], scales[:, cols], values)
 
-        passes_done = {}
+        def blocks_in_bank(c):
+            return CHUNKS // 2 if c == LAST else CHUNKS
 
         def moment(f_chunks, c, groups):
             g_codes, g_scales = weighted_mx[G_MAP, c]
+            blocks = blocks_in_bank(c)
             for g in groups:
                 cols = slice(g * P, (g + 1) * P)
                 for i in f_chunks:
-                    blocks = 2 if c == CHUNKS - 1 else CHUNKS
                     key = (c, i // blocks)
-                    if key not in moment_banks:
-                        moment_banks[key] = new_held_bank() if c < 2 else new_bank()
+                    if key not in out_banks:
+                        out_banks[key] = new_held_bank() if c < HELD_BANKS else new_bank()
                         passes_done[key] = 0
                     f_codes, f_scales = weighted_mx[F_MAP, i]
                     nc.tensor.matmul_mx(
-                        out=moment_banks[key][:, (i % blocks) * P : (i % blocks + 1) * P],
+                        out=out_banks[key][:, (i % blocks) * P : (i % blocks + 1) * P],
                         lhsT=f_codes[:, cols].bitcast(FP8X4),
                         lhsT_scale=f_scales[:, cols],
                         rhs=g_codes[:, cols].bitcast(FP8X4),
@@ -344,34 +348,28 @@ def tile_twolobeweightedkoopmancrossmoment_kernel(tc, x, y_bytes, y_scale, w0, w
                     )
                     passes_done[key] += 1
 
-        def store(c, side, on_vector):
-            blocks = 2 if c == CHUNKS - 1 else CHUNKS
-            result = work.tile([P, blocks * P], F32, name="values", bufs=6, align_bytes=64)
-            bank = moment_banks[c, side][:, 0 : blocks * P]
-            if on_vector:
-                nc.vector.tensor_scalar(out=result[:], in0=bank, scalar1=1.0 / math.sqrt(N), scalar2=None, op0=ALU.mult)
-            else:
-                nc.scalar.activation(out=result[:], in_=bank, func=ACT.Copy, scale=1.0 / math.sqrt(N))
-            rows = slice(side * blocks * P, (side + 1) * blocks * P)
+        def scale_on_vector(result, bank):
+            nc.vector.tensor_scalar(out=result, in0=bank, scalar1=1.0 / math.sqrt(N), scalar2=None, op0=ALU.mult)
+
+        def scale_on_scalar(result, bank):
+            nc.scalar.activation(out=result, in_=bank, func=ACT.Copy, scale=1.0 / math.sqrt(N))
+
+        def store(c, part, scale):
+            width = blocks_in_bank(c) * P
+            result = new_staging(width, F32)
+            scale(result[:], out_banks[c, part][:, 0:width])
             nc.sync.dma_start(
-                out=out[rows, c * P : (c + 1) * P].rearrange("(i q) k -> q i k", q=P),
+                out=out[part * width : (part + 1) * width, c * P : (c + 1) * P].rearrange("(i q) k -> q i k", q=P),
                 in_=result[:].rearrange("q (i k) -> q i k", k=P),
             )
 
-        every = range(GROUPS)
-        widen_y(0)
-        turn_rows(F_MAP, 0)
-        turn_rows(G_MAP, 0)
+        all_groups, all_chunks = range(GROUPS), range(CHUNKS)
+
         interleave_w(F_MAP)
-        widen_y(1)
-        turn_rows(F_MAP, 1)
-        turn_rows(G_MAP, 1)
-        widen_y(2)
-        turn_rows(G_MAP, 2)
-        turn_rows(F_MAP, 2)
-        turn_rows(F_MAP, 3)
-        widen_y(3)
-        turn_rows(G_MAP, 3)
+        for h in range(4):
+            widen_y(h)
+        for fmap, h in ((F_MAP, 0), (G_MAP, 0), (F_MAP, 1), (G_MAP, 1), (G_MAP, 2), (F_MAP, 2), (F_MAP, 3), (G_MAP, 3)):
+            turn_rows(fmap, h)
         quantize_rows(F_MAP, 0)
         quantize_w(F_MAP)
         quantize_rows(F_MAP, 1)
@@ -379,72 +377,73 @@ def tile_twolobeweightedkoopmancrossmoment_kernel(tc, x, y_bytes, y_scale, w0, w
         turn_rows(F_MAP, 4)
         turn_rows(F_MAP, 5)
         quantize_rows(F_MAP, 2)
+
         interleave_w(G_MAP)
+        for h in range(4, 7):
+            widen_y(h)
         feature_group(F_MAP, 0)
-        widen_y(4)
         turn_rows(F_MAP, 6)
         turn_rows(F_MAP, 7)
-        widen_y(5)
         feature_group(F_MAP, 1)
-        widen_y(6)
         quantize_rows(F_MAP, 3)
         quantize_rows(G_MAP, 1)
         quantize_w(G_MAP)
         feature_group(F_MAP, 2)
         turn_rows(G_MAP, 4)
-        last_feature_group(F_MAP)
-        weigh_f_on_gpsimd(0, range(0, 3))
+        for c in all_chunks:
+            feature_chunk(F_MAP, GROUPS - 1, c)
+            if c > 0:
+                take_mean(F_MAP, c - 1)
+        take_mean(F_MAP, LAST)
+
+        weigh_f_on_gpsimd(0, GPSIMD_GROUPS)
         turn_rows(G_MAP, 5)
         widen_y(7)
-        p_rows = [spread(p_cols, 0)]
+        p_banks = [spread(p_columns, 0)]
         turn_rows(G_MAP, 6)
-        p_rows.append(spread(p_cols, 1))
-        weigh_f(1, every)
-        feature_chunk(G_MAP, 0, 0)
-        feature_chunk(G_MAP, 1, 0)
-        turn_rows(G_MAP, 7)
-        weigh_f(2, every)
-        quantize_rows(G_MAP, 2)
-        quantize_rows(G_MAP, 3)
-        for c in range(1, CHUNKS):
+        p_banks.append(spread(p_columns, 1))
+        weigh_f(1, all_groups, p_banks)
+        weigh_f(2, all_groups, p_banks)
+        for c in all_chunks:
             feature_chunk(G_MAP, 0, c)
             feature_chunk(G_MAP, 1, c)
-        weigh_f(0, range(3, 4))
-        weigh_f(3, every)
-        for c in range(CHUNKS):
+            if c == 0:
+                turn_rows(G_MAP, 7)
+        quantize_rows(G_MAP, 2)
+        quantize_rows(G_MAP, 3)
+        weigh_f(0, range(len(GPSIMD_GROUPS), GROUPS), p_banks)
+        weigh_f(LAST, all_groups, p_banks)
+
+        for c in all_chunks:
             feature_chunk(G_MAP, 2, c)
             feature_chunk(G_MAP, 3, c)
             turn_weighted(F_MAP, c, range(0, 2))
-            mean(G_MAP, c)
+            take_mean(G_MAP, c)
             turn_weighted(F_MAP, c, range(2, 4))
             if c > 0:
-                turn_weighted(G_MAP, c - 1, every)
-            if c == 2:
-                moment(range(0, 2), 0, every)
-            if c == 3:
-                moment(range(2, 3), 0, every)
-                moment(range(0, 3), 1, every)
-                weigh_g(c, range(0, 2))
-            else:
-                weigh_g(c, every)
-            quantize_weighted(F_MAP, c, every)
+                turn_weighted(G_MAP, c - 1, all_groups)
+            for earlier in range(c - 1):
+                moment(range(0, c) if earlier == c - 2 else [c - 1], earlier, all_groups)
+            weigh_g(c, all_groups if c < LAST else range(0, 2))
+            quantize_weighted(F_MAP, c, all_groups)
             if c > 0:
-                quantize_weighted(G_MAP, c - 1, every)
-        turn_weighted(G_MAP, 3, range(0, 2))
-        moment(range(3, 4), 0, every)
-        moment(range(3, 4), 1, every)
-        weigh_g(3, range(2, 3))
-        weigh_g(3, range(3, 4))
-        store(0, 0, False)
-        moment(every, 2, range(0, 2))
-        turn_weighted(G_MAP, 3, range(2, 3))
-        turn_weighted(G_MAP, 3, range(3, 4))
-        quantize_weighted(G_MAP, 3, range(0, 2))
-        store(1, 0, True)
-        moment(every, 2, range(2, 4))
-        quantize_weighted(G_MAP, 3, range(2, 3))
-        quantize_weighted(G_MAP, 3, range(3, 4))
-        moment(every, 3, every)
-        store(2, 0, False)
-        store(3, 0, True)
-        store(3, 1, False)
+                quantize_weighted(G_MAP, c - 1, all_groups)
+
+        turn_weighted(G_MAP, LAST, range(0, 2))
+        moment([LAST], 0, all_groups)
+        moment([LAST], 1, all_groups)
+        weigh_g(LAST, [2])
+        weigh_g(LAST, [3])
+        store(0, 0, scale_on_scalar)
+        moment(all_chunks, 2, range(0, 2))
+        turn_weighted(G_MAP, LAST, [2])
+        turn_weighted(G_MAP, LAST, [3])
+        quantize_weighted(G_MAP, LAST, range(0, 2))
+        store(1, 0, scale_on_vector)
+        moment(all_chunks, 2, range(2, 4))
+        quantize_weighted(G_MAP, LAST, [2])
+        quantize_weighted(G_MAP, LAST, [3])
+        moment(all_chunks, LAST, all_groups)
+        store(2, 0, scale_on_scalar)
+        store(LAST, 0, scale_on_vector)
+        store(LAST, 1, scale_on_scalar)

import math
from contextlib import ExitStack

import concourse.mybir as mybir
from concourse.masks import make_identity

N, D, K = 2048, 1024, 512
FLOPS = 2 * (2 * N * D * K) + 2 * N * K * K

F32 = mybir.dt.float32
BF16 = mybir.dt.bfloat16
U32 = mybir.dt.uint32
U8 = mybir.dt.uint8
FP8 = mybir.dt.float8_e4m3fn
FP8X4 = mybir.dt.float8_e4m3fn_x4
ALU = mybir.AluOpType
ACT = mybir.ActivationFunctionType

P = 128
PACK = 4
PASS = P * PACK
HALF = PASS // 2
D_PASSES = D // PASS
GROUPS = N // PASS
CHUNKS = K // P
LAST = CHUNKS - 1
F_MAP, G_MAP = 0, 1
STREAM = ("x", "y")

HELD_BANKS = 2
TURNING_BANKS = 6
STAGING_BUFS = 6
PAIR_BUFS = 2
CODE_BUFS = (3, 4)
GPSIMD_GROUPS = range(0, 3)
GPSIMD_ROWS = len(GPSIMD_GROUPS) * PASS


def tile_twolobeweightedkoopmancrossmoment_kernel(tc, x, y_bytes, y_scale, w0, w1, b, p, a, out):
    nc = tc.nc
    with ExitStack() as ctx:
        keep = ctx.enter_context(tc.tile_pool(name="keep", bufs=1))
        work = ctx.enter_context(tc.tile_pool(name="work", bufs=2))
        psum = ctx.enter_context(tc.psum_pool(name="psum", bufs=TURNING_BANKS))
        ctx.enter_context(tc.manual_schedule())

        def new_bank():
            return psum.tile([P, PASS], F32, name="bank")

        def new_held_bank():
            return psum.tile([P, PASS], F32, name="held_bank", bufs=HELD_BANKS)

        def new_staging(columns, dtype):
            return work.tile([P, columns], dtype, name="staging", bufs=STAGING_BUFS, align_bytes=64)

        def new_pairs(fmap):
            return work.tile([P, 2048], F32, name="pairs_" + STREAM[fmap], bufs=PAIR_BUFS, align_bytes=64)

        def new_gpsimd_buffer():
            return work.tile([P, 2048], F32, name="gpsimd_buffer", bufs=1, align_bytes=64)

        def new_codes(fmap):
            bufs = CODE_BUFS[fmap]
            codes = work.tile([P, 2 * PASS], U32, name="codes_" + STREAM[fmap], bufs=bufs, align_bytes=64)
            scales = work.tile([P, 2 * PASS], U8, name="scales_" + STREAM[fmap], bufs=bufs, align_bytes=64)
            return codes, scales

        def new_wide(columns, dtype):
            return work.tile([P, columns], dtype, name="wide", bufs=2 * CHUNKS, align_bytes=256)

        def quantize(codes, scales, values):
            nc.vector.quantize_mx(out=codes.bitcast(FP8X4), scales=scales, in_=values)

        w_rows, x_rows, y_rows, row_weight = {}, {}, {}, {}

        def load_columns(name, vector):
            columns = keep.tile([P, 2 * PACK], F32, name=name)
            nc.sync.dma_start(
                out=columns[:].rearrange("q (j t) -> q j t", t=PACK),
                in_=vector.rearrange("(j q t) -> q j t", q=P, t=PACK),
            )
            return columns

        def load_w(fmap, j):
            if j == 0:
                both_passes = new_wide(D_PASSES * PACK * K, BF16)
                for i in range(D_PASSES):
                    w_rows[fmap, i] = both_passes[:, i * PACK * K : (i + 1) * PACK * K]
            rows = (w0, w1)[fmap][j * PASS : (j + 1) * PASS, :]
            nc.sync.dma_start(out=w_rows[fmap, j], in_=rows.rearrange("(q t) k -> q (t k)", t=PACK))

        def load_x(h):
            x_rows[h] = keep.tile([P, 2 * D], BF16, name="x_rows_%d" % h, align_bytes=256)
            rows = x[h * HALF : (h + 1) * HALF, :]
            nc.sync.dma_start(out=x_rows[h][:], in_=rows.rearrange("(r u) d -> r (u d)", u=2))

        def load_y(h):
            y_rows[h] = keep.tile([P, 2 * D], U8, name="y_byte_rows_%d" % h, align_bytes=256)
            rows = y_bytes[h * HALF : (h + 1) * HALF, :]
            nc.sync.dma_start(out=y_rows[h][:], in_=rows.rearrange("(r u) d -> r (u d)", u=2))

        def load_row_weight(fmap, rows):
            row_weight[fmap] = keep.tile([P, rows], BF16, name="row_weight_%d" % fmap, align_bytes=256)
            nc.sync.dma_start(out=row_weight[fmap][:], in_=(p, a)[fmap][0:rows].partition_broadcast(P))

        scale_columns = load_columns("scale_columns", y_scale.rearrange("o d -> (o d)"))
        load_y(0)
        bias_rows = keep.tile([2 * CHUNKS, P], BF16)
        nc.sync.dma_start(out=bias_rows[:], in_=b.rearrange("l (c q) -> (l c) q", q=P))
        for j in range(D_PASSES):
            load_x(j)
            load_y(j + 1)
            load_w(F_MAP, j)
        load_y(3)
        for h in range(2, 6):
            load_x(h)
        load_w(G_MAP, 0)
        load_y(4)
        load_w(G_MAP, 1)
        for h in range(6, 8):
            load_x(h)
            load_y(h - 1)
        load_y(7)
        p_columns = load_columns("p_columns", p.bitcast(F32))
        load_row_weight(F_MAP, GPSIMD_ROWS)
        load_row_weight(G_MAP, N)

        ident = keep.tile([P, P], F32)
        make_identity(nc, ident[:])
        bias_square = keep.tile([P, P], F32)
        nc.gpsimd.memset(bias_square[:], 0.0)
        nc.scalar.activation(out=bias_square[0 : 2 * CHUNKS, :], in_=bias_rows[:], func=ACT.Copy)

        def spread(columns, j):
            bank = new_held_bank()
            for t in range(PACK):
                nc.tensor.transpose(
                    bank[:].rearrange("r (q t) -> r q t", t=PACK)[:, :, t],
                    columns[:, PACK * j + t : PACK * j + t + 1].to_broadcast([P, P]),
                    ident[:],
                )
            return bank

        scale_banks = [spread(scale_columns, j) for j in range(D_PASSES)]

        bias = keep.tile([P, 2 * CHUNKS], F32)
        bias_bank = new_bank()
        nc.tensor.transpose(bias_bank[:, 0:P], bias_square[:], ident[:])
        nc.scalar.copy(out=bias[:], in_=bias_bank[:, 0 : 2 * CHUNKS])

        w_values, w_mx, y_values, row_pairs, row_mx, features = {}, {}, {}, {}, {}, {}

        def interleave_w(fmap):
            w_values[fmap] = new_gpsimd_buffer()[:].bitcast(BF16)
            for j in range(D_PASSES):
                nc.gpsimd.tensor_scalar(
                    out=w_values[fmap][:, j * PACK * K : (j + 1) * PACK * K].rearrange("q (k t) -> q k t", t=PACK),
                    in0=w_rows[fmap, j].rearrange("q (t k) -> q k t", t=PACK),
                    scalar1=1.0,
                    scalar2=0.0,
                    op0=ALU.mult,
                    op1=ALU.add,
                )

        def quantize_w(fmap):
            codes = keep.tile([P, D_PASSES * K], U32, name="w_codes_%d" % fmap, align_bytes=64)
            scales = keep.tile([P, D_PASSES * K], U8, name="w_scales_%d" % fmap, align_bytes=64)
            quantize(codes[:], scales[:], w_values[fmap])
            w_mx[fmap] = (codes, scales)

        def widen_y(h):
            y_values[h] = new_staging(2 * D, BF16)
            for j in range(D_PASSES):
                for u in range(2):
                    cols = slice(u * D + j * PASS, u * D + (j + 1) * PASS)
                    nc.vector.tensor_tensor(
                        out=y_values[h][:, cols],
                        in0=y_rows[h][:, cols].bitcast(FP8),
                        in1=scale_banks[j][:],
                        op=ALU.mult,
                    )

        def turn_rows(fmap, h):
            g, side = divmod(h, 2)
            source = (x_rows, y_values)[fmap][h][:].bitcast(F32)
            if side == 0:
                row_pairs[fmap, g] = new_gpsimd_buffer() if (fmap, g) == (F_MAP, 2) else new_pairs(fmap)
            target = row_pairs[fmap, g][:].rearrange("q (j u s r v) -> q j s u r v", j=D_PASSES, u=2, s=2, v=2)
            for j in range(D_PASSES):
                bank = new_bank()
                for u in range(2):
                    first = u * (D // 2) + j * HALF
                    for v in range(2):
                        nc.tensor.transpose(
                            bank[:, (2 * u + v) * P : (2 * u + v + 1) * P],
                            source[:, first + v : first + HALF : 2],
                            ident[:],
                        )
                nc.scalar.copy(out=target[:, j, side, :, :, :], in_=bank[:].rearrange("q (u v r) -> q u r v", u=2, v=2))

        def quantize_rows(fmap, g):
            row_mx[fmap, g] = new_codes(fmap)
            codes, scales = row_mx[fmap, g]
            quantize(codes[:], scales[:], row_pairs[fmap, g][:].bitcast(BF16))

        group_sums = keep.tile([P, 2 * CHUNKS * GROUPS], F32)
        minus_mean = keep.tile([P, 2 * CHUNKS], F32)

        def by_parity(tile, groups):
            return tile[:].rearrange("q (u m) -> q u m", u=2)[:, :, groups[0] * HALF : (groups[-1] + 1) * HALF]

        def feature_chunk(fmap, g, c):
            bank = new_bank()
            w_codes, w_scales = w_mx[fmap]
            row_codes, row_scales = row_mx[fmap, g]
            for j in range(D_PASSES):
                w_cols = slice(j * K + c * P, j * K + (c + 1) * P)
                row_cols = slice(j * PASS, (j + 1) * PASS)
                nc.tensor.matmul_mx(
                    out=bank[:],
                    lhsT=w_codes[:, w_cols].bitcast(FP8X4),
                    lhsT_scale=w_scales[:, w_cols],
                    rhs=row_codes[:, row_cols].bitcast(FP8X4),
                    rhs_scale=row_scales[:, row_cols],
                    start=(j == 0),
                    stop=(j == D_PASSES - 1),
                )
            col = fmap * CHUNKS + c
            if g == 0:
                features[fmap, c] = new_wide(N, F32)
            nc.scalar.activation(
                out=by_parity(features[fmap, c], [g]),
                in_=bank[:].rearrange("q (u m) -> q u m", u=2),
                func=ACT.Tanh,
                bias=bias[:, col : col + 1],
                accum_out=group_sums[:, col * GROUPS + g : col * GROUPS + g + 1],
            )

        def feature_group(fmap, g):
            for c in range(CHUNKS):
                feature_chunk(fmap, g, c)

        def take_mean(fmap, c):
            col = fmap * CHUNKS + c
            parts = group_sums[:, col * GROUPS : (col + 1) * GROUPS]
            nc.scalar.activation(
                out=parts, in_=parts, func=ACT.Copy, scale=-1.0 / N, accum_out=minus_mean[:, col : col + 1]
            )

        weighted, weighted_pairs, weighted_mx, out_banks, passes_done = {}, {}, {}, {}, {}

        def weights_by_parity(weights, first_group, groups):
            span = slice((groups[0] - first_group) * HALF, (groups[-1] + 1 - first_group) * HALF)
            return weights.rearrange("q (m u) -> q u m", u=2)[:, :, span]

        def weigh(fmap, c, groups, weights):
            if (fmap, c) not in weighted:
                weighted[fmap, c] = new_staging(N, BF16)
            col = fmap * CHUNKS + c
            nc.vector.scalar_tensor_tensor(
                out=by_parity(weighted[fmap, c], groups),
                in0=by_parity(features[fmap, c], groups),
                scalar=minus_mean[:, col : col + 1],
                in1=weights,
                op0=ALU.add,
                op1=ALU.mult,
            )

        def weigh_g(c, groups):
            weigh(G_MAP, c, groups, weights_by_parity(row_weight[G_MAP][:], 0, groups))

        def weigh_f(c, groups, p_banks):
            for j in sorted(set(g // 2 for g in groups)):
                part = [g for g in groups if g // 2 == j]
                weigh(F_MAP, c, part, weights_by_parity(p_banks[j][:].bitcast(BF16), 2 * j, part))

        def weigh_f_on_gpsimd(c, groups):
            weighted[F_MAP, c] = new_staging(N, BF16)
            centred = new_gpsimd_buffer()
            nc.gpsimd.tensor_scalar(
                out=by_parity(centred, groups),
                in0=by_parity(features[F_MAP, c], groups),
                scalar1=minus_mean[:, c : c + 1],
                scalar2=1.0,
                op0=ALU.add,
                op1=ALU.mult,
            )
            nc.gpsimd.tensor_tensor(
                out=by_parity(weighted[F_MAP, c], groups),
                in0=by_parity(centred, groups),
                in1=weights_by_parity(row_weight[F_MAP][:], 0, groups),
                op=ALU.mult,
            )

        def turn_weighted(fmap, c, groups):
            source = weighted[fmap, c][:].bitcast(F32)
            if (fmap, c) not in weighted_pairs:
                two_chunks = new_pairs(fmap)
                weighted_pairs[fmap, c] = two_chunks[:, 0 : N // 2]
                weighted_pairs[fmap, c + 1] = two_chunks[:, N // 2 : N]
            for first_group in groups[::2]:
                count = min(2, groups[-1] + 1 - first_group)
                bank = new_bank()
                for s in range(count):
                    for u in range(2):
                        first = u * (N // 4) + (first_group + s) * P
                        nc.tensor.transpose(
                            bank[:, (2 * s + u) * P : (2 * s + u + 1) * P], source[:, first : first + P], ident[:]
                        )
                target = weighted_pairs[fmap, c][:, first_group * HALF : (first_group + count) * HALF]
                nc.scalar.copy(
                    out=target.rearrange("q (s k u) -> q s k u", s=count, u=2),
                    in_=bank[:, 0 : count * HALF].rearrange("q (s u k) -> q s k u", s=count, u=2),
                )

        def quantize_weighted(fmap, c, groups):
            if (fmap, c) not in weighted_mx:
                two_chunks = new_codes(fmap)
                weighted_mx[fmap, c] = [part[:, 0:PASS] for part in two_chunks]
                weighted_mx[fmap, c + 1] = [part[:, PASS : 2 * PASS] for part in two_chunks]
            codes, scales = weighted_mx[fmap, c]
            cols = slice(groups[0] * P, (groups[-1] + 1) * P)
            values = weighted_pairs[fmap, c].bitcast(BF16)[:, groups[0] * PASS : (groups[-1] + 1) * PASS]
            quantize(codes[:, cols], scales[:, cols], values)

        def blocks_in_bank(c):
            return CHUNKS // 2 if c == LAST else CHUNKS

        def moment(f_chunks, c, groups):
            g_codes, g_scales = weighted_mx[G_MAP, c]
            blocks = blocks_in_bank(c)
            for g in groups:
                cols = slice(g * P, (g + 1) * P)
                for i in f_chunks:
                    key = (c, i // blocks)
                    if key not in out_banks:
                        out_banks[key] = new_held_bank() if c < HELD_BANKS else new_bank()
                        passes_done[key] = 0
                    f_codes, f_scales = weighted_mx[F_MAP, i]
                    nc.tensor.matmul_mx(
                        out=out_banks[key][:, (i % blocks) * P : (i % blocks + 1) * P],
                        lhsT=f_codes[:, cols].bitcast(FP8X4),
                        lhsT_scale=f_scales[:, cols],
                        rhs=g_codes[:, cols].bitcast(FP8X4),
                        rhs_scale=g_scales[:, cols],
                        start=(passes_done[key] == 0),
                        stop=(passes_done[key] == blocks * GROUPS - 1),
                    )
                    passes_done[key] += 1

        def scale_on_vector(result, bank):
            nc.vector.tensor_scalar(out=result, in0=bank, scalar1=1.0 / math.sqrt(N), scalar2=None, op0=ALU.mult)

        def scale_on_scalar(result, bank):
            nc.scalar.activation(out=result, in_=bank, func=ACT.Copy, scale=1.0 / math.sqrt(N))

        def store(c, part, scale):
            width = blocks_in_bank(c) * P
            result = new_staging(width, F32)
            scale(result[:], out_banks[c, part][:, 0:width])
            nc.sync.dma_start(
                out=out[part * width : (part + 1) * width, c * P : (c + 1) * P].rearrange("(i q) k -> q i k", q=P),
                in_=result[:].rearrange("q (i k) -> q i k", k=P),
            )

        all_groups, all_chunks = range(GROUPS), range(CHUNKS)

        interleave_w(F_MAP)
        for h in range(4):
            widen_y(h)
        for fmap, h in ((F_MAP, 0), (G_MAP, 0), (F_MAP, 1), (G_MAP, 1), (G_MAP, 2), (F_MAP, 2), (F_MAP, 3), (G_MAP, 3)):
            turn_rows(fmap, h)
        quantize_rows(F_MAP, 0)
        quantize_w(F_MAP)
        quantize_rows(F_MAP, 1)
        quantize_rows(G_MAP, 0)
        turn_rows(F_MAP, 4)
        turn_rows(F_MAP, 5)
        quantize_rows(F_MAP, 2)

        interleave_w(G_MAP)
        for h in range(4, 7):
            widen_y(h)
        feature_group(F_MAP, 0)
        turn_rows(F_MAP, 6)
        turn_rows(F_MAP, 7)
        feature_group(F_MAP, 1)
        quantize_rows(F_MAP, 3)
        quantize_rows(G_MAP, 1)
        quantize_w(G_MAP)
        feature_group(F_MAP, 2)
        turn_rows(G_MAP, 4)
        for c in all_chunks:
            feature_chunk(F_MAP, GROUPS - 1, c)
            if c > 0:
                take_mean(F_MAP, c - 1)
        take_mean(F_MAP, LAST)

        weigh_f_on_gpsimd(0, GPSIMD_GROUPS)
        turn_rows(G_MAP, 5)
        widen_y(7)
        p_banks = [spread(p_columns, 0)]
        turn_rows(G_MAP, 6)
        p_banks.append(spread(p_columns, 1))
        weigh_f(1, all_groups, p_banks)
        weigh_f(2, all_groups, p_banks)
        for c in all_chunks:
            feature_chunk(G_MAP, 0, c)
            feature_chunk(G_MAP, 1, c)
            if c == 0:
                turn_rows(G_MAP, 7)
        quantize_rows(G_MAP, 2)
        quantize_rows(G_MAP, 3)
        weigh_f(0, range(len(GPSIMD_GROUPS), GROUPS), p_banks)
        weigh_f(LAST, all_groups, p_banks)

        for c in all_chunks:
            feature_chunk(G_MAP, 2, c)
            feature_chunk(G_MAP, 3, c)
            turn_weighted(F_MAP, c, range(0, 2))
            take_mean(G_MAP, c)
            turn_weighted(F_MAP, c, range(2, 4))
            if c > 0:
                turn_weighted(G_MAP, c - 1, all_groups)
            for earlier in range(c - 1):
                moment(range(0, c) if earlier == c - 2 else [c - 1], earlier, all_groups)
            weigh_g(c, all_groups if c < LAST else range(0, 2))
            quantize_weighted(F_MAP, c, all_groups)
            if c > 0:
                quantize_weighted(G_MAP, c - 1, all_groups)

        turn_weighted(G_MAP, LAST, range(0, 2))
        moment([LAST], 0, all_groups)
        moment([LAST], 1, all_groups)
        weigh_g(LAST, [2])
        weigh_g(LAST, [3])
        store(0, 0, scale_on_scalar)
        moment(all_chunks, 2, range(0, 2))
        turn_weighted(G_MAP, LAST, [2])
        turn_weighted(G_MAP, LAST, [3])
        quantize_weighted(G_MAP, LAST, range(0, 2))
        store(1, 0, scale_on_vector)
        moment(all_chunks, 2, range(2, 4))
        quantize_weighted(G_MAP, LAST, [2])
        quantize_weighted(G_MAP, LAST, [3])
        moment(all_chunks, LAST, all_groups)
        store(2, 0, scale_on_scalar)
        store(LAST, 0, scale_on_vector)
        store(LAST, 1, scale_on_scalar)
